import numpy as np
import ml_dtypes


def mxq(x, axis, fmt="e4m3"):
    dtype, down = {"e4m3": (ml_dtypes.float8_e4m3fn, 7), "e5m2": (ml_dtypes.float8_e5m2, 14)}[fmt]
    v = np.moveaxis(np.asarray(x, np.float32).astype(ml_dtypes.bfloat16).astype(np.float64), axis, -1)
    blocks = v.reshape(v.shape[:-1] + (-1, 32))
    amax = np.abs(blocks).max(-1, keepdims=True)
    byte = np.maximum(np.where(amax > 0, np.frexp(amax)[1] - 1 + 127, 0) - down, 1)
    scale = np.exp2(byte - 127.0)
    codes = (blocks / scale).astype(np.float32).astype(dtype).astype(np.float64)
    return np.moveaxis((codes * scale).reshape(v.shape), -1, axis)


WIDE = False


def mx_kscale(k):
    if not WIDE:
        return np.ones(k)
    levels = np.array([10, -10, 5, -5, 0])
    if k % 512:
        return np.exp2(np.random.permutation(np.resize(levels, k // 32))).repeat(32)
    a = np.empty((k // 512, 16))
    for p in range(k // 512):
        a[p, :8] = np.random.permutation(np.resize(levels, 8))
        for g in range(8):
            far = levels[np.abs(levels - a[p, g]) >= 10]
            a[p, g + 8] = far[np.random.randint(len(far))]
    return np.exp2(a.ravel()).repeat(32)


def f64(x):
    return np.asarray(x).astype(np.float64)


def striped(idx):
    return np.tile(np.asarray(idx).reshape(-1, 16).T, (8, 1)).astype(np.uint16)


def unstriped(offs):
    return offs[:16].T.reshape(-1).astype(np.int64)


E2M1 = np.array([0.0, 0.5, 1.0, 1.5, 2.0, 3.0, 4.0, 6.0, -0.0, -0.5, -1.0, -1.5, -2.0, -3.0, -4.0, -6.0])


def pack_weight(w, fmt):
    k, n = w.shape
    w = f64(np.asarray(w, np.float32).astype(ml_dtypes.bfloat16)).reshape(k // 32, 32, n)
    amax = np.abs(w).max(1)
    if fmt == "e4m3":
        byte = np.frexp(amax)[1] - 1 + 127 - 7
    else:
        mant, ex = np.frexp(amax / 6.0)
        byte = np.where(mant > 0.5, ex, ex - 1) + 127
    byte = np.clip(np.where(amax > 0, byte, 1), 1, 254)
    scaled = (w * np.exp2(127.0 - byte)[:, None, :]).reshape(k, n).astype(np.float32)
    by_word = np.ascontiguousarray(scaled.reshape(k // 512, 128, 4, n).transpose(0, 1, 3, 2))
    if fmt == "e4m3":
        words = by_word.astype(ml_dtypes.float8_e4m3fn).view(np.uint8)
    else:
        c = by_word.astype(ml_dtypes.float4_e2m1fn).view(np.uint8) & 0xF
        words = (c[..., 0::2] | (c[..., 1::2] << 4)).reshape(k // 512, 128, 2 * n)
    return np.ascontiguousarray(words), np.ascontiguousarray(byte.astype(np.uint8).reshape(k // 512, 16, n))


def unpack_weight(words, scales, fmt):
    g, _, n = scales.shape
    words = np.ascontiguousarray(words).reshape(g, 128, n, -1)
    if fmt == "e4m3":
        vals = words.view(ml_dtypes.float8_e4m3fn).astype(np.float64)
    else:
        nib = np.empty((g, 128, n, 4), np.uint8)
        nib[..., 0::2] = words & 0xF
        nib[..., 1::2] = words >> 4
        vals = E2M1[nib]
    vals = vals * np.repeat(np.exp2(scales.astype(np.float64) - 127.0), 8, axis=1)[..., None]
    return vals.transpose(0, 1, 3, 2).reshape(g * 512, n)


def silu(v):
    return v / (1.0 + np.exp(-v))


B, N, T, D, NQ = 1, 512, 2048, 512, 128


def setup_inputs():
    n = np.random.standard_normal
    idx = np.random.permutation(T)[:B * N]
    s = mx_kscale(D)[:, None]
    kp = pack_weight(n((D, T)) / s, "e4m3")
    cp = pack_weight(n((D, T)) / s, "e4m3")
    return {
        "qT": (n((B, D, NQ)) * s * (1.00 / np.sqrt(D))).astype(np.float32),
        "k_words": kp[0],
        "k_scales": kp[1],
        "c_words": cp[0],
        "c_scales": cp[1],
        "offs": striped(idx),
    }


def reference(qT, k_words, k_scales, c_words, c_scales, offs):
    idx = unstriped(offs)
    pick = lambda x, which: x[:, which].reshape(x.shape[0], B, -1).transpose(1, 0, 2)
    k = unpack_weight(k_words, k_scales, "e4m3")
    kg = pick(k, idx)
    c = unpack_weight(c_words, c_scales, "e4m3")
    cg = pick(c, idx)
    qq = mxq(f64(qT), 1, "e4m3")
    a = qq.transpose(0, 2, 1) @ kg
    z = qq.transpose(0, 2, 1) @ cg
    y = silu(a) * z
    out = np.zeros((B, NQ, T))
    for b in range(B):
        out[b][:, idx[b * N:(b + 1) * N]] = y[b]
    return out

@@ -1,0 +1,80 @@
+from contextlib import ExitStack
+
+import concourse.mybir as mybir
+
+P, PACK, T, N, NQ = 128, 4, 2048, 512, 128
+HALF = N // 2
+F32, BF16 = mybir.dt.float32, mybir.dt.bfloat16
+I32, U32, U16, U8 = mybir.dt.int32, mybir.dt.uint32, mybir.dt.uint16, mybir.dt.uint8
+FP8X4 = mybir.dt.float8_e4m3fn_x4
+ACT = mybir.ActivationFunctionType
+FLOPS = 2 * 2 * NQ * 512 * N
+
+
+def tile_attend_neu_swigluscat_topk_kernel(tc, qT, k_words, k_scales, c_words, c_scales, offs, out):
+    nc = tc.nc
+    with ExitStack() as ctx:
+        sb = ctx.enter_context(tc.tile_pool(name="sb", bufs=1))
+        ps = ctx.enter_context(tc.psum_pool(name="ps", bufs=1))
+
+        offsets = sb.tile([P, N // 16], U16, name="offsets")
+        ks_all = sb.tile([P, T], U8, name="ks_all", align_bytes=64)
+        cs_all = sb.tile([P, T], U8, name="cs_all", align_bytes=64)
+        kw_all = sb.tile([P, T], I32, name="kw_all", align_bytes=64)
+        cw_all = sb.tile([P, T], I32, name="cw_all", align_bytes=64)
+        q_raw = sb.tile([P, PACK, NQ], F32, name="q_raw", align_bytes=64)
+        placed = sb.tile([P, T], F32, name="placed", align_bytes=64)
+        warm_in = sb.tile([P, 8], F32, name="warm_in")
+        warm_out = sb.tile([P, 8], F32, name="warm_out")
+
+        nc.vector.memset(ks_all[:].bitcast(I32), 0)
+        nc.vector.memset(cs_all[:].bitcast(I32), 0)
+        nc.gpsimd.memset(warm_in[:], 0.0)
+
+        nc.sync.dma_start(offsets[:], offs)
+        for first, tile_all, src in ((0, ks_all, k_scales), (4, cs_all, c_scales)):
+            rows = src[0].bitcast(I32)
+            for quad in range(4):
+                lo = 32 * quad + first
+                nc.scalar.dma_start(tile_all[lo : lo + 4, :].bitcast(I32), rows[4 * quad : 4 * quad + 4, :])
+        nc.sync.dma_start(kw_all[:], k_words[0].rearrange("p n t -> p (n t)").bitcast(I32))
+        nc.sync.dma_start(q_raw[:], qT[0].rearrange("(p j) w -> p j w", j=PACK))
+        nc.sync.dma_start(cw_all[:], c_words[0].rearrange("p n t -> p (n t)").bitcast(I32))
+
+        nc.scalar.activation(warm_out[:], warm_in[:], ACT.Silu)
+        nc.vector.memset(placed[:], 0.0)
+
+        ks = sb.tile([P, N], U8, name="ks", align_bytes=64)
+        cs = sb.tile([P, N], U8, name="cs", align_bytes=64)
+        kw = sb.tile([P, N], U32, name="kw", align_bytes=64)
+        nc.vector.tensor_copy(ks[:], ks_all[:].indirect(offsets[:]))
+        nc.vector.tensor_copy(cs[:], cs_all[:].indirect(offsets[:]))
+        nc.vector.tensor_copy(kw[:], kw_all[:].bitcast(U32).indirect(offsets[:]))
+
+        q_bf = sb.tile([P, NQ, PACK], BF16, name="q_bf", align_bytes=64)
+        qw = sb.tile([P, NQ], U32, name="qw", align_bytes=64)
+        qs = sb.tile([P, NQ], U8, name="qs", align_bytes=64)
+        nc.scalar.copy(q_bf[:], q_raw[:].rearrange("p j w -> p w j"))
+        nc.vector.quantize_mx(out=qw[:].bitcast(FP8X4), scales=qs[:], in_=q_bf[:].rearrange("p w j -> p (w j)"))
+
+        a_ps = ps.tile([P, N], F32, name="a_ps")
+        nc.tensor.matmul_mx(out=a_ps[:], lhsT=qw[:].bitcast(FP8X4), lhsT_scale=qs[:],
+                            rhs=kw[:].bitcast(FP8X4), rhs_scale=ks[:], start=True, stop=True)
+        gate = sb.tile([P, N], F32, name="gate", align_bytes=64)
+        nc.scalar.activation(gate[:], a_ps[:], ACT.Silu)
+
+        halves = [(h, slice(h * HALF, (h + 1) * HALF), offsets[:, h * HALF // 16 : (h + 1) * HALF // 16]) for h in range(2)]
+        z_ps = []
+        for h, cols, offs_h in halves:
+            cw = sb.tile([P, HALF], U32, name=f"cw{h}", align_bytes=64)
+            nc.vector.tensor_copy(cw[:], cw_all[:].bitcast(U32).indirect(offs_h))
+            z = ps.tile([P, HALF], F32, name=f"z{h}")
+            nc.tensor.matmul_mx(out=z[:], lhsT=qw[:].bitcast(FP8X4), lhsT_scale=qs[:],
+                                rhs=cw[:].bitcast(FP8X4), rhs_scale=cs[4:P, cols], start=True, stop=True)
+            z_ps.append(z)
+        for h, cols, offs_h in halves:
+            y = sb.tile([P, HALF], F32, name=f"y{h}", align_bytes=64)
+            nc.vector.tensor_tensor(y[:], z_ps[h][:], gate[:, cols], mybir.AluOpType.mult)
+            nc.vector.tensor_copy(placed[:].indirect(offs_h), y[:])
+
+        nc.sync.dma_start(out[0], placed[:])

@@ -21,35 +21,33 @@ def tile_attend_neu_swigluscat_topk_kernel(tc, qT, k_words, k_scales, c_words, c
         ks_all = sb.tile([P, T], U8, name="ks_all", align_bytes=64)
         cs_all = sb.tile([P, T], U8, name="cs_all", align_bytes=64)
         kw_all = sb.tile([P, T], I32, name="kw_all", align_bytes=64)
-        cw_all = sb.tile([P, T], I32, name="cw_all", align_bytes=64)
         q_raw = sb.tile([P, PACK, NQ], F32, name="q_raw", align_bytes=64)
         placed = sb.tile([P, T], F32, name="placed", align_bytes=64)
-        warm_in = sb.tile([P, 8], F32, name="warm_in")
-        warm_out = sb.tile([P, 8], F32, name="warm_out")
+        warm_out = sb.tile([P, 8], F32, name="warm_out", tag="late", align_bytes=64)
 
         nc.vector.memset(ks_all[:].bitcast(I32), 0)
         nc.vector.memset(cs_all[:].bitcast(I32), 0)
-        nc.gpsimd.memset(warm_in[:], 0.0)
+        nc.vector.memset(placed[:], 0.0)
 
         nc.sync.dma_start(offsets[:], offs)
         for first, tile_all, src in ((0, ks_all, k_scales), (4, cs_all, c_scales)):
             rows = src[0].bitcast(I32)
             for quad in range(4):
                 lo = 32 * quad + first
-                nc.scalar.dma_start(tile_all[lo : lo + 4, :].bitcast(I32), rows[4 * quad : 4 * quad + 4, :])
+                queue = nc.gpsimd if (first and quad >= 2) else nc.scalar
+                queue.dma_start(tile_all[lo : lo + 4, :].bitcast(I32), rows[4 * quad : 4 * quad + 4, :])
         nc.sync.dma_start(kw_all[:], k_words[0].rearrange("p n t -> p (n t)").bitcast(I32))
         nc.sync.dma_start(q_raw[:], qT[0].rearrange("(p j) w -> p j w", j=PACK))
+        nc.scalar.activation(warm_out[:], placed[:, 0:8], ACT.Silu)
+        cw_all = sb.tile([P, T], I32, name="cw_all", tag="late", align_bytes=64)
         nc.sync.dma_start(cw_all[:], c_words[0].rearrange("p n t -> p (n t)").bitcast(I32))
-
-        nc.scalar.activation(warm_out[:], warm_in[:], ACT.Silu)
-        nc.vector.memset(placed[:], 0.0)
 
         ks = sb.tile([P, N], U8, name="ks", align_bytes=64)
         cs = sb.tile([P, N], U8, name="cs", align_bytes=64)
         kw = sb.tile([P, N], U32, name="kw", align_bytes=64)
+        nc.vector.tensor_copy(kw[:], kw_all[:].bitcast(U32).indirect(offsets[:]))
         nc.vector.tensor_copy(ks[:], ks_all[:].indirect(offsets[:]))
         nc.vector.tensor_copy(cs[:], cs_all[:].indirect(offsets[:]))
-        nc.vector.tensor_copy(kw[:], kw_all[:].bitcast(U32).indirect(offsets[:]))
 
         q_bf = sb.tile([P, NQ, PACK], BF16, name="q_bf", align_bytes=64)
         qw = sb.tile([P, NQ], U32, name="qw", align_bytes=64)

@@ -72,7 +72,7 @@ def tile_attend_neu_swigluscat_topk_kernel(tc, qT, k_words, k_scales, c_words, c
             z_ps.append(z)
         for h, cols, offs_h in halves:
             y = sb.tile([P, HALF], F32, name=f"y{h}", align_bytes=64)
-            nc.vector.tensor_tensor(y[:], z_ps[h][:], gate[:, cols], mybir.AluOpType.mult)
-            nc.vector.tensor_copy(placed[:].indirect(offs_h), y[:])
+            nc.scalar.copy(y[:], z_ps[h][:])
+            nc.vector.tensor_tensor(placed[:].indirect(offs_h), gate[:, cols], y[:], mybir.AluOpType.mult)
 
         nc.sync.dma_start(out[0], placed[:])

@@ -43,13 +43,11 @@ def tile_attend_neu_swigluscat_topk_kernel(tc, qT, k_words, k_scales, c_words, c
         nc.sync.dma_start(cw_all[:], c_words[0].rearrange("p n t -> p (n t)").bitcast(I32))
 
         ks = sb.tile([P, N], U8, name="ks", align_bytes=64)
-        cs = sb.tile([P, N], U8, name="cs", align_bytes=64)
         kw = sb.tile([P, N], U32, name="kw", align_bytes=64)
         nc.vector.tensor_copy(kw[:], kw_all[:].bitcast(U32).indirect(offsets[:]))
         nc.vector.tensor_copy(ks[:], ks_all[:].indirect(offsets[:]))
-        nc.vector.tensor_copy(cs[:], cs_all[:].indirect(offsets[:]))
 
-        q_bf = sb.tile([P, NQ, PACK], BF16, name="q_bf", align_bytes=64)
+        q_bf = sb.tile([P, NQ, PACK], BF16, name="q_bf", tag="q_then_cs", align_bytes=64)
         qw = sb.tile([P, NQ], U32, name="qw", align_bytes=64)
         qs = sb.tile([P, NQ], U8, name="qs", align_bytes=64)
         nc.scalar.copy(q_bf[:], q_raw[:].rearrange("p j w -> p w j"))
@@ -61,18 +59,23 @@ def tile_attend_neu_swigluscat_topk_kernel(tc, qT, k_words, k_scales, c_words, c
         gate = sb.tile([P, N], F32, name="gate", align_bytes=64)
         nc.scalar.activation(gate[:], a_ps[:], ACT.Silu)
 
-        halves = [(h, slice(h * HALF, (h + 1) * HALF), offsets[:, h * HALF // 16 : (h + 1) * HALF // 16]) for h in range(2)]
-        z_ps = []
-        for h, cols, offs_h in halves:
+        cs = sb.tile([P, N], U8, name="cs", tag="q_then_cs", align_bytes=64)
+        nc.vector.tensor_copy(cs[:], cs_all[:].indirect(offsets[:]))
+
+        offs_h = [offsets[:, h * HALF // 16 : (h + 1) * HALF // 16] for h in range(2)]
+        ys = []
+        for h in range(2):
             cw = sb.tile([P, HALF], U32, name=f"cw{h}", align_bytes=64)
-            nc.vector.tensor_copy(cw[:], cw_all[:].bitcast(U32).indirect(offs_h))
-            z = ps.tile([P, HALF], F32, name=f"z{h}")
-            nc.tensor.matmul_mx(out=z[:], lhsT=qw[:].bitcast(FP8X4), lhsT_scale=qs[:],
-                                rhs=cw[:].bitcast(FP8X4), rhs_scale=cs[4:P, cols], start=True, stop=True)
-            z_ps.append(z)
-        for h, cols, offs_h in halves:
+            nc.vector.tensor_copy(cw[:], cw_all[:].bitcast(U32).indirect(offs_h[h]))
             y = sb.tile([P, HALF], F32, name=f"y{h}", align_bytes=64)
-            nc.scalar.copy(y[:], z_ps[h][:])
-            nc.vector.tensor_tensor(placed[:].indirect(offs_h), gate[:, cols], y[:], mybir.AluOpType.mult)
+            for piece in range(2):
+                cols = slice(piece * P, (piece + 1) * P)
+                z = ps.tile([P, P], F32, name=f"z{h}{piece}")
+                nc.tensor.matmul_mx(out=z[:], lhsT=qw[:].bitcast(FP8X4), lhsT_scale=qs[:], rhs=cw[:, cols].bitcast(FP8X4),
+                                    rhs_scale=cs[4:P, h * HALF + piece * P : h * HALF + (piece + 1) * P], start=True, stop=True)
+                nc.scalar.copy(y[:, cols], z[:])
+            ys.append(y)
+        for h, y in enumerate(ys):
+            nc.vector.tensor_tensor(placed[:].indirect(offs_h[h]), gate[:, h * HALF : (h + 1) * HALF], y[:], mybir.AluOpType.mult)
 
         nc.sync.dma_start(out[0], placed[:])

@@ -18,40 +18,44 @@ def tile_attend_neu_swigluscat_topk_kernel(tc, qT, k_words, k_scales, c_words, c
         ps = ctx.enter_context(tc.psum_pool(name="ps", bufs=1))
 
         offsets = sb.tile([P, N // 16], U16, name="offsets")
-        ks_all = sb.tile([P, T], U8, name="ks_all", align_bytes=64)
+        ks_all = sb.tile([P, T], U8, name="ks_all", tag="ks_then_cs", align_bytes=64)
         cs_all = sb.tile([P, T], U8, name="cs_all", align_bytes=64)
         kw_all = sb.tile([P, T], I32, name="kw_all", align_bytes=64)
         q_raw = sb.tile([P, PACK, NQ], F32, name="q_raw", align_bytes=64)
-        placed = sb.tile([P, T], F32, name="placed", align_bytes=64)
-        warm_out = sb.tile([P, 8], F32, name="warm_out", tag="late", align_bytes=64)
+        warm_in = sb.tile([P, 8], F32, name="warm_in", align_bytes=64)
+        warm_out = sb.tile([P, 8], F32, name="warm_out", tag="warm_then_cw", align_bytes=64)
 
-        nc.vector.memset(ks_all[:].bitcast(I32), 0)
         nc.vector.memset(cs_all[:].bitcast(I32), 0)
-        nc.vector.memset(placed[:], 0.0)
+        nc.vector.memset(ks_all[:].bitcast(I32), 0)
+        nc.vector.memset(warm_in[:], 0.0)
 
         nc.sync.dma_start(offsets[:], offs)
-        for first, tile_all, src in ((0, ks_all, k_scales), (4, cs_all, c_scales)):
-            rows = src[0].bitcast(I32)
-            for quad in range(4):
-                lo = 32 * quad + first
-                queue = nc.gpsimd if (first and quad >= 2) else nc.scalar
-                queue.dma_start(tile_all[lo : lo + 4, :].bitcast(I32), rows[4 * quad : 4 * quad + 4, :])
-        nc.sync.dma_start(kw_all[:], k_words[0].rearrange("p n t -> p (n t)").bitcast(I32))
         nc.sync.dma_start(q_raw[:], qT[0].rearrange("(p j) w -> p j w", j=PACK))
-        nc.scalar.activation(warm_out[:], placed[:, 0:8], ACT.Silu)
-        cw_all = sb.tile([P, T], I32, name="cw_all", tag="late", align_bytes=64)
+        nc.sync.dma_start(kw_all[:], k_words[0].rearrange("p n t -> p (n t)").bitcast(I32))
+        c_rows = c_scales[0].bitcast(I32)
+        for quad in range(4):
+            lo = 32 * quad + 4
+            queue = nc.gpsimd if quad >= 2 else nc.scalar
+            queue.dma_start(cs_all[lo : lo + 4, :].bitcast(I32), c_rows[4 * quad : 4 * quad + 4, :])
+        k_rows = k_scales[0].bitcast(I32)
+        for r in range(4):
+            nc.scalar.dma_start(ks_all[r:P:32, :].bitcast(I32), k_rows[r:16:4, :])
+        nc.scalar.activation(warm_out[:], warm_in[:], ACT.Silu)
+        cw_all = sb.tile([P, T], I32, name="cw_all", tag="warm_then_cw", align_bytes=64)
         nc.sync.dma_start(cw_all[:], c_words[0].rearrange("p n t -> p (n t)").bitcast(I32))
 
-        ks = sb.tile([P, N], U8, name="ks", align_bytes=64)
-        kw = sb.tile([P, N], U32, name="kw", align_bytes=64)
-        nc.vector.tensor_copy(kw[:], kw_all[:].bitcast(U32).indirect(offsets[:]))
-        nc.vector.tensor_copy(ks[:], ks_all[:].indirect(offsets[:]))
-
-        q_bf = sb.tile([P, NQ, PACK], BF16, name="q_bf", tag="q_then_cs", align_bytes=64)
+        q_bf = sb.tile([P, NQ, PACK], BF16, name="q_bf", tag="q_then_out", align_bytes=64)
         qw = sb.tile([P, NQ], U32, name="qw", align_bytes=64)
         qs = sb.tile([P, NQ], U8, name="qs", align_bytes=64)
-        nc.scalar.copy(q_bf[:], q_raw[:].rearrange("p j w -> p w j"))
+        nc.vector.tensor_copy(q_bf[:], q_raw[:].rearrange("p j w -> p w j"))
         nc.vector.quantize_mx(out=qw[:].bitcast(FP8X4), scales=qs[:], in_=q_bf[:].rearrange("p w j -> p (w j)"))
+        placed = sb.tile([P, T], F32, name="placed", tag="q_then_out", align_bytes=64)
+        nc.vector.memset(placed[:], 0.0)
+
+        kw = sb.tile([P, N], U32, name="kw", align_bytes=64)
+        ks = sb.tile([P, N], U8, name="ks", align_bytes=64)
+        nc.vector.tensor_copy(kw[:], kw_all[:].bitcast(U32).indirect(offsets[:]))
+        nc.vector.tensor_copy(ks[:], ks_all[:].indirect(offsets[:]))
 
         a_ps = ps.tile([P, N], F32, name="a_ps")
         nc.tensor.matmul_mx(out=a_ps[:], lhsT=qw[:].bitcast(FP8X4), lhsT_scale=qs[:],
@@ -59,23 +63,26 @@ def tile_attend_neu_swigluscat_topk_kernel(tc, qT, k_words, k_scales, c_words, c
         gate = sb.tile([P, N], F32, name="gate", align_bytes=64)
         nc.scalar.activation(gate[:], a_ps[:], ACT.Silu)
 
-        cs = sb.tile([P, N], U8, name="cs", tag="q_then_cs", align_bytes=64)
-        nc.vector.tensor_copy(cs[:], cs_all[:].indirect(offsets[:]))
+        def product(h, cw, cs):
+            z = ps.tile([P, HALF], F32, name=f"z{h}")
+            nc.tensor.matmul_mx(out=z[:], lhsT=qw[:].bitcast(FP8X4), lhsT_scale=qs[:],
+                                rhs=cw[:].bitcast(FP8X4), rhs_scale=cs[4:P, :], start=True, stop=True)
+            y = sb.tile([P, HALF], F32, name=f"y{h}", align_bytes=64)
+            nc.scalar.copy(y[:], z[:])
+            return y
 
         offs_h = [offsets[:, h * HALF // 16 : (h + 1) * HALF // 16] for h in range(2)]
-        ys = []
-        for h in range(2):
-            cw = sb.tile([P, HALF], U32, name=f"cw{h}", align_bytes=64)
-            nc.vector.tensor_copy(cw[:], cw_all[:].bitcast(U32).indirect(offs_h[h]))
-            y = sb.tile([P, HALF], F32, name=f"y{h}", align_bytes=64)
-            for piece in range(2):
-                cols = slice(piece * P, (piece + 1) * P)
-                z = ps.tile([P, P], F32, name=f"z{h}{piece}")
-                nc.tensor.matmul_mx(out=z[:], lhsT=qw[:].bitcast(FP8X4), lhsT_scale=qs[:], rhs=cw[:, cols].bitcast(FP8X4),
-                                    rhs_scale=cs[4:P, h * HALF + piece * P : h * HALF + (piece + 1) * P], start=True, stop=True)
-                nc.scalar.copy(y[:, cols], z[:])
-            ys.append(y)
-        for h, y in enumerate(ys):
+        cs0 = sb.tile([P, HALF], U8, name="cs0", tag="ks_then_cs", align_bytes=64)
+        cw0 = sb.tile([P, HALF], U32, name="cw0", tag="cw_then_cs", align_bytes=64)
+        cw1 = sb.tile([P, HALF], U32, name="cw1", align_bytes=64)
+        nc.vector.tensor_copy(cs0[:], cs_all[:].indirect(offs_h[0]))
+        nc.vector.tensor_copy(cw0[:], cw_all[:].bitcast(U32).indirect(offs_h[0]))
+        nc.vector.tensor_copy(cw1[:], cw_all[:].bitcast(U32).indirect(offs_h[1]))
+        y0 = product(0, cw0, cs0)
+        cs1 = sb.tile([P, HALF], U8, name="cs1", tag="cw_then_cs", align_bytes=64)
+        nc.vector.tensor_copy(cs1[:], cs_all[:].indirect(offs_h[1]))
+        y1 = product(1, cw1, cs1)
+        for h, y in enumerate((y0, y1)):
             nc.vector.tensor_tensor(placed[:].indirect(offs_h[h]), gate[:, h * HALF : (h + 1) * HALF], y[:], mybir.AluOpType.mult)
 
         nc.sync.dma_start(out[0], placed[:])

@@ -15,19 +15,20 @@ def tile_attend_neu_swigluscat_topk_kernel(tc, qT, k_words, k_scales, c_words, c
     nc = tc.nc
     with ExitStack() as ctx:
         sb = ctx.enter_context(tc.tile_pool(name="sb", bufs=1))
+        reuse = ctx.enter_context(tc.tile_pool(name="reuse", bufs=1))
         ps = ctx.enter_context(tc.psum_pool(name="ps", bufs=1))
 
         offsets = sb.tile([P, N // 16], U16, name="offsets")
         ks_all = sb.tile([P, T], U8, name="ks_all", tag="ks_then_cs", align_bytes=64)
         cs_all = sb.tile([P, T], U8, name="cs_all", align_bytes=64)
         kw_all = sb.tile([P, T], I32, name="kw_all", align_bytes=64)
-        q_raw = sb.tile([P, PACK, NQ], F32, name="q_raw", align_bytes=64)
-        warm_in = sb.tile([P, 8], F32, name="warm_in", align_bytes=64)
-        warm_out = sb.tile([P, 8], F32, name="warm_out", tag="warm_then_cw", align_bytes=64)
+        q_raw = reuse.tile([P, PACK, NQ], F32, name="q_raw", align_bytes=64, offset=0)
+        placed = sb.tile([P, T], F32, name="placed", align_bytes=64)
 
         nc.vector.memset(cs_all[:].bitcast(I32), 0)
         nc.vector.memset(ks_all[:].bitcast(I32), 0)
-        nc.vector.memset(warm_in[:], 0.0)
+        nc.vector.memset(placed[:, : T // 2 - 1], 0.0)
+        nc.vector.memset(placed[:, T // 2 - 1 :], 0.0)
 
         nc.sync.dma_start(offsets[:], offs)
         nc.sync.dma_start(q_raw[:], qT[0].rearrange("(p j) w -> p j w", j=PACK))
@@ -40,17 +41,14 @@ def tile_attend_neu_swigluscat_topk_kernel(tc, qT, k_words, k_scales, c_words, c
         k_rows = k_scales[0].bitcast(I32)
         for r in range(4):
             nc.scalar.dma_start(ks_all[r:P:32, :].bitcast(I32), k_rows[r:16:4, :])
-        nc.scalar.activation(warm_out[:], warm_in[:], ACT.Silu)
-        cw_all = sb.tile([P, T], I32, name="cw_all", tag="warm_then_cw", align_bytes=64)
-        nc.sync.dma_start(cw_all[:], c_words[0].rearrange("p n t -> p (n t)").bitcast(I32))
 
-        q_bf = sb.tile([P, NQ, PACK], BF16, name="q_bf", tag="q_then_out", align_bytes=64)
+        q_bf = sb.tile([P, NQ, PACK], BF16, name="q_bf", align_bytes=64)
         qw = sb.tile([P, NQ], U32, name="qw", align_bytes=64)
         qs = sb.tile([P, NQ], U8, name="qs", align_bytes=64)
         nc.vector.tensor_copy(q_bf[:], q_raw[:].rearrange("p j w -> p w j"))
         nc.vector.quantize_mx(out=qw[:].bitcast(FP8X4), scales=qs[:], in_=q_bf[:].rearrange("p w j -> p (w j)"))
-        placed = sb.tile([P, T], F32, name="placed", tag="q_then_out", align_bytes=64)
-        nc.vector.memset(placed[:], 0.0)
+        cw_all = reuse.tile([P, T], I32, name="cw_all", align_bytes=64, offset=0)
+        nc.sync.dma_start(cw_all[:], c_words[0].rearrange("p n t -> p (n t)").bitcast(I32))
 
         kw = sb.tile([P, N], U32, name="kw", align_bytes=64)
         ks = sb.tile([P, N], U8, name="ks", align_bytes=64)
@@ -73,13 +71,13 @@ def tile_attend_neu_swigluscat_topk_kernel(tc, qT, k_words, k_scales, c_words, c
 
         offs_h = [offsets[:, h * HALF // 16 : (h + 1) * HALF // 16] for h in range(2)]
         cs0 = sb.tile([P, HALF], U8, name="cs0", tag="ks_then_cs", align_bytes=64)
-        cw0 = sb.tile([P, HALF], U32, name="cw0", tag="cw_then_cs", align_bytes=64)
+        cw0 = sb.tile([P, HALF], U32, name="cw0", align_bytes=64)
         cw1 = sb.tile([P, HALF], U32, name="cw1", align_bytes=64)
         nc.vector.tensor_copy(cs0[:], cs_all[:].indirect(offs_h[0]))
         nc.vector.tensor_copy(cw0[:], cw_all[:].bitcast(U32).indirect(offs_h[0]))
         nc.vector.tensor_copy(cw1[:], cw_all[:].bitcast(U32).indirect(offs_h[1]))
         y0 = product(0, cw0, cs0)
-        cs1 = sb.tile([P, HALF], U8, name="cs1", tag="cw_then_cs", align_bytes=64)
+        cs1 = reuse.tile([P, HALF], U8, name="cs1", align_bytes=64, offset=0)
         nc.vector.tensor_copy(cs1[:], cs_all[:].indirect(offs_h[1]))
         y1 = product(1, cw1, cs1)
         for h, y in enumerate((y0, y1)):

@@ -19,28 +19,29 @@ def tile_attend_neu_swigluscat_topk_kernel(tc, qT, k_words, k_scales, c_words, c
         ps = ctx.enter_context(tc.psum_pool(name="ps", bufs=1))
 
         offsets = sb.tile([P, N // 16], U16, name="offsets")
-        ks_all = sb.tile([P, T], U8, name="ks_all", tag="ks_then_cs", align_bytes=64)
+        ks_all = sb.tile([P, T], U8, name="ks_all", align_bytes=64)
         cs_all = sb.tile([P, T], U8, name="cs_all", align_bytes=64)
         kw_all = sb.tile([P, T], I32, name="kw_all", align_bytes=64)
         q_raw = reuse.tile([P, PACK, NQ], F32, name="q_raw", align_bytes=64, offset=0)
         placed = sb.tile([P, T], F32, name="placed", align_bytes=64)
 
-        nc.vector.memset(cs_all[:].bitcast(I32), 0)
+        nc.vector.memset(cs_all[P // 2 :, :].bitcast(I32), 0)
         nc.vector.memset(ks_all[:].bitcast(I32), 0)
+        nc.vector.memset(cs_all[: P // 2, :].bitcast(I32), 0)
         nc.vector.memset(placed[:, : T // 2 - 1], 0.0)
         nc.vector.memset(placed[:, T // 2 - 1 :], 0.0)
 
         nc.sync.dma_start(offsets[:], offs)
         nc.sync.dma_start(q_raw[:], qT[0].rearrange("(p j) w -> p j w", j=PACK))
         nc.sync.dma_start(kw_all[:], k_words[0].rearrange("p n t -> p (n t)").bitcast(I32))
+        k_rows = k_scales[0].bitcast(I32)
+        for r in range(4):
+            nc.scalar.dma_start(ks_all[r:P:32, :].bitcast(I32), k_rows[r:16:4, :])
         c_rows = c_scales[0].bitcast(I32)
         for quad in range(4):
             lo = 32 * quad + 4
             queue = nc.gpsimd if quad >= 2 else nc.scalar
             queue.dma_start(cs_all[lo : lo + 4, :].bitcast(I32), c_rows[4 * quad : 4 * quad + 4, :])
-        k_rows = k_scales[0].bitcast(I32)
-        for r in range(4):
-            nc.scalar.dma_start(ks_all[r:P:32, :].bitcast(I32), k_rows[r:16:4, :])
 
         q_bf = sb.tile([P, NQ, PACK], BF16, name="q_bf", align_bytes=64)
         qw = sb.tile([P, NQ], U32, name="qw", align_bytes=64)
@@ -70,7 +71,7 @@ def tile_attend_neu_swigluscat_topk_kernel(tc, qT, k_words, k_scales, c_words, c
             return y
 
         offs_h = [offsets[:, h * HALF // 16 : (h + 1) * HALF // 16] for h in range(2)]
-        cs0 = sb.tile([P, HALF], U8, name="cs0", tag="ks_then_cs", align_bytes=64)
+        cs0 = sb.tile([P, HALF], U8, name="cs0", align_bytes=64)
         cw0 = sb.tile([P, HALF], U32, name="cw0", align_bytes=64)
         cw1 = sb.tile([P, HALF], U32, name="cw1", align_bytes=64)
         nc.vector.tensor_copy(cs0[:], cs_all[:].indirect(offs_h[0]))

@@ -22,39 +22,36 @@ def tile_attend_neu_swigluscat_topk_kernel(tc, qT, k_words, k_scales, c_words, c
         ks_all = sb.tile([P, T], U8, name="ks_all", align_bytes=64)
         cs_all = sb.tile([P, T], U8, name="cs_all", align_bytes=64)
         kw_all = sb.tile([P, T], I32, name="kw_all", align_bytes=64)
-        q_raw = reuse.tile([P, PACK, NQ], F32, name="q_raw", align_bytes=64, offset=0)
+        q_raw = sb.tile([P, PACK, NQ], F32, name="q_raw", align_bytes=64)
+        cw_all = reuse.tile([P, T], I32, name="cw_all", align_bytes=64, offset=0)
         placed = sb.tile([P, T], F32, name="placed", align_bytes=64)
 
-        nc.vector.memset(cs_all[P // 2 :, :].bitcast(I32), 0)
         nc.vector.memset(ks_all[:].bitcast(I32), 0)
-        nc.vector.memset(cs_all[: P // 2, :].bitcast(I32), 0)
-        nc.vector.memset(placed[:, : T // 2 - 1], 0.0)
-        nc.vector.memset(placed[:, T // 2 - 1 :], 0.0)
+        nc.vector.memset(cs_all[:].bitcast(I32), 0)
+        nc.vector.memset(placed[:], 0.0)
 
+        k_rows = k_scales[0].bitcast(I32)
+        c_rows = c_scales[0].bitcast(I32)
         nc.sync.dma_start(offsets[:], offs)
         nc.sync.dma_start(q_raw[:], qT[0].rearrange("(p j) w -> p j w", j=PACK))
-        nc.sync.dma_start(kw_all[:], k_words[0].rearrange("p n t -> p (n t)").bitcast(I32))
-        k_rows = k_scales[0].bitcast(I32)
         for r in range(4):
-            nc.scalar.dma_start(ks_all[r:P:32, :].bitcast(I32), k_rows[r:16:4, :])
-        c_rows = c_scales[0].bitcast(I32)
-        for quad in range(4):
-            lo = 32 * quad + 4
-            queue = nc.gpsimd if quad >= 2 else nc.scalar
-            queue.dma_start(cs_all[lo : lo + 4, :].bitcast(I32), c_rows[4 * quad : 4 * quad + 4, :])
+            queue = nc.sync if r < 2 else nc.scalar
+            queue.dma_start(ks_all[r:P:32, :].bitcast(I32), k_rows[r:16:4, :])
+        nc.sync.dma_start(kw_all[:], k_words[0].rearrange("p n t -> p (n t)").bitcast(I32))
+        for r in range(4):
+            nc.sync.dma_start(cs_all[4 + r : P : 32, :].bitcast(I32), c_rows[r:16:4, :])
+        nc.sync.dma_start(cw_all[:], c_words[0].rearrange("p n t -> p (n t)").bitcast(I32))
 
         q_bf = sb.tile([P, NQ, PACK], BF16, name="q_bf", align_bytes=64)
         qw = sb.tile([P, NQ], U32, name="qw", align_bytes=64)
         qs = sb.tile([P, NQ], U8, name="qs", align_bytes=64)
         nc.vector.tensor_copy(q_bf[:], q_raw[:].rearrange("p j w -> p w j"))
         nc.vector.quantize_mx(out=qw[:].bitcast(FP8X4), scales=qs[:], in_=q_bf[:].rearrange("p w j -> p (w j)"))
-        cw_all = reuse.tile([P, T], I32, name="cw_all", align_bytes=64, offset=0)
-        nc.sync.dma_start(cw_all[:], c_words[0].rearrange("p n t -> p (n t)").bitcast(I32))
 
         kw = sb.tile([P, N], U32, name="kw", align_bytes=64)
         ks = sb.tile([P, N], U8, name="ks", align_bytes=64)
-        nc.vector.tensor_copy(kw[:], kw_all[:].bitcast(U32).indirect(offsets[:]))
         nc.vector.tensor_copy(ks[:], ks_all[:].indirect(offsets[:]))
+        nc.vector.tensor_copy(kw[:], kw_all[:].bitcast(U32).indirect(offsets[:]))
 
         a_ps = ps.tile([P, N], F32, name="a_ps")
         nc.tensor.matmul_mx(out=a_ps[:], lhsT=qw[:].bitcast(FP8X4), lhsT_scale=qs[:],

@@ -4,6 +4,7 @@ import concourse.mybir as mybir
 
 P, PACK, T, N, NQ = 128, 4, 2048, 512, 128
 HALF = N // 2
+LEAD = T // 4
 F32, BF16 = mybir.dt.float32, mybir.dt.bfloat16
 I32, U32, U16, U8 = mybir.dt.int32, mybir.dt.uint32, mybir.dt.uint16, mybir.dt.uint8
 FP8X4 = mybir.dt.float8_e4m3fn_x4
@@ -15,7 +16,6 @@ def tile_attend_neu_swigluscat_topk_kernel(tc, qT, k_words, k_scales, c_words, c
     nc = tc.nc
     with ExitStack() as ctx:
         sb = ctx.enter_context(tc.tile_pool(name="sb", bufs=1))
-        reuse = ctx.enter_context(tc.tile_pool(name="reuse", bufs=1))
         ps = ctx.enter_context(tc.psum_pool(name="ps", bufs=1))
 
         offsets = sb.tile([P, N // 16], U16, name="offsets")
@@ -23,7 +23,7 @@ def tile_attend_neu_swigluscat_topk_kernel(tc, qT, k_words, k_scales, c_words, c
         cs_all = sb.tile([P, T], U8, name="cs_all", align_bytes=64)
         kw_all = sb.tile([P, T], I32, name="kw_all", align_bytes=64)
         q_raw = sb.tile([P, PACK, NQ], F32, name="q_raw", align_bytes=64)
-        cw_all = reuse.tile([P, T], I32, name="cw_all", align_bytes=64, offset=0)
+        cw_all = sb.tile([P, T], I32, name="cw_all", align_bytes=64)
         placed = sb.tile([P, T], F32, name="placed", align_bytes=64)
 
         nc.vector.memset(ks_all[:].bitcast(I32), 0)
@@ -38,9 +38,11 @@ def tile_attend_neu_swigluscat_topk_kernel(tc, qT, k_words, k_scales, c_words, c
             queue = nc.sync if r < 2 else nc.scalar
             queue.dma_start(ks_all[r:P:32, :].bitcast(I32), k_rows[r:16:4, :])
         nc.sync.dma_start(kw_all[:], k_words[0].rearrange("p n t -> p (n t)").bitcast(I32))
+        c_src = c_words[0].rearrange("p n t -> p (n t)").bitcast(I32)
+        nc.sync.dma_start(cw_all[:, :LEAD], c_src[:, :LEAD])
         for r in range(4):
             nc.sync.dma_start(cs_all[4 + r : P : 32, :].bitcast(I32), c_rows[r:16:4, :])
-        nc.sync.dma_start(cw_all[:], c_words[0].rearrange("p n t -> p (n t)").bitcast(I32))
+        nc.sync.dma_start(cw_all[:, LEAD:], c_src[:, LEAD:])
 
         q_bf = sb.tile([P, NQ, PACK], BF16, name="q_bf", align_bytes=64)
         qw = sb.tile([P, NQ], U32, name="qw", align_bytes=64)
@@ -59,25 +61,25 @@ def tile_attend_neu_swigluscat_topk_kernel(tc, qT, k_words, k_scales, c_words, c
         gate = sb.tile([P, N], F32, name="gate", align_bytes=64)
         nc.scalar.activation(gate[:], a_ps[:], ACT.Silu)
 
-        def product(h, cw, cs):
-            z = ps.tile([P, HALF], F32, name=f"z{h}")
+        def product(y, lo, width, cw):
+            z = ps.tile([P, width], F32, name=f"z{lo}")
+            at = lo % HALF
             nc.tensor.matmul_mx(out=z[:], lhsT=qw[:].bitcast(FP8X4), lhsT_scale=qs[:],
-                                rhs=cw[:].bitcast(FP8X4), rhs_scale=cs[4:P, :], start=True, stop=True)
-            y = sb.tile([P, HALF], F32, name=f"y{h}", align_bytes=64)
-            nc.scalar.copy(y[:], z[:])
-            return y
+                                rhs=cw[:, at : at + width].bitcast(FP8X4), rhs_scale=cs[4:P, lo : lo + width], start=True, stop=True)
+            nc.scalar.copy(y[:, at : at + width], z[:])
 
         offs_h = [offsets[:, h * HALF // 16 : (h + 1) * HALF // 16] for h in range(2)]
-        cs0 = sb.tile([P, HALF], U8, name="cs0", align_bytes=64)
+        cs = sb.tile([P, N], U8, name="cs", align_bytes=64)
         cw0 = sb.tile([P, HALF], U32, name="cw0", align_bytes=64)
         cw1 = sb.tile([P, HALF], U32, name="cw1", align_bytes=64)
-        nc.vector.tensor_copy(cs0[:], cs_all[:].indirect(offs_h[0]))
+        y0 = sb.tile([P, HALF], F32, name="y0", align_bytes=64)
+        y1 = sb.tile([P, HALF], F32, name="y1", align_bytes=64)
+        nc.vector.tensor_copy(cs[:], cs_all[:].indirect(offsets[:]))
         nc.vector.tensor_copy(cw0[:], cw_all[:].bitcast(U32).indirect(offs_h[0]))
         nc.vector.tensor_copy(cw1[:], cw_all[:].bitcast(U32).indirect(offs_h[1]))
-        y0 = product(0, cw0, cs0)
-        cs1 = reuse.tile([P, HALF], U8, name="cs1", align_bytes=64, offset=0)
-        nc.vector.tensor_copy(cs1[:], cs_all[:].indirect(offs_h[1]))
-        y1 = product(1, cw1, cs1)
+        product(y0, 0, HALF // 2, cw0)
+        product(y0, HALF // 2, HALF // 2, cw0)
+        product(y1, HALF, HALF, cw1)
         for h, y in enumerate((y0, y1)):
             nc.vector.tensor_tensor(placed[:].indirect(offs_h[h]), gate[:, h * HALF : (h + 1) * HALF], y[:], mybir.AluOpType.mult)
 

@@ -4,7 +4,7 @@ import concourse.mybir as mybir
 
 P, PACK, T, N, NQ = 128, 4, 2048, 512, 128
 HALF = N // 2
-LEAD = T // 4
+LEAD = T // 8
 F32, BF16 = mybir.dt.float32, mybir.dt.bfloat16
 I32, U32, U16, U8 = mybir.dt.int32, mybir.dt.uint32, mybir.dt.uint16, mybir.dt.uint8
 FP8X4 = mybir.dt.float8_e4m3fn_x4
@@ -28,59 +28,58 @@ def tile_attend_neu_swigluscat_topk_kernel(tc, qT, k_words, k_scales, c_words, c
 
         nc.vector.memset(ks_all[:].bitcast(I32), 0)
         nc.vector.memset(cs_all[:].bitcast(I32), 0)
+        k_plane = sb.tile([P, N], U8, name="k_plane", align_bytes=64)
+        c_plane = sb.tile([P, N], U8, name="c_plane", align_bytes=64)
+        nc.vector.memset(k_plane[:].bitcast(I32), 0)
         nc.vector.memset(placed[:], 0.0)
 
-        k_rows = k_scales[0].bitcast(I32)
-        c_rows = c_scales[0].bitcast(I32)
         nc.sync.dma_start(offsets[:], offs)
+        k_src = k_words[0].rearrange("p n t -> p (n t)").bitcast(I32)
+        nc.sync.dma_start(kw_all[:, :LEAD], k_src[:, :LEAD])
+        nc.sync.dma_start(ks_all[0:P:8, :].bitcast(I32), k_scales[0].bitcast(I32))
         nc.sync.dma_start(q_raw[:], qT[0].rearrange("(p j) w -> p j w", j=PACK))
-        for r in range(4):
-            queue = nc.sync if r < 2 else nc.scalar
-            queue.dma_start(ks_all[r:P:32, :].bitcast(I32), k_rows[r:16:4, :])
-        nc.sync.dma_start(kw_all[:], k_words[0].rearrange("p n t -> p (n t)").bitcast(I32))
-        c_src = c_words[0].rearrange("p n t -> p (n t)").bitcast(I32)
-        nc.sync.dma_start(cw_all[:, :LEAD], c_src[:, :LEAD])
-        for r in range(4):
-            nc.sync.dma_start(cs_all[4 + r : P : 32, :].bitcast(I32), c_rows[r:16:4, :])
-        nc.sync.dma_start(cw_all[:, LEAD:], c_src[:, LEAD:])
+        nc.sync.dma_start(cs_all[4:P:8, :].bitcast(I32), c_scales[0].bitcast(I32))
+        nc.sync.dma_start(kw_all[:, LEAD:], k_src[:, LEAD:])
+        nc.sync.dma_start(cw_all[:], c_words[0].rearrange("p n t -> p (n t)").bitcast(I32))
 
         q_bf = sb.tile([P, NQ, PACK], BF16, name="q_bf", align_bytes=64)
         qw = sb.tile([P, NQ], U32, name="qw", align_bytes=64)
         qs = sb.tile([P, NQ], U8, name="qs", align_bytes=64)
-        nc.vector.tensor_copy(q_bf[:], q_raw[:].rearrange("p j w -> p w j"))
-        nc.vector.quantize_mx(out=qw[:].bitcast(FP8X4), scales=qs[:], in_=q_bf[:].rearrange("p w j -> p (w j)"))
-
-        kw = sb.tile([P, N], U32, name="kw", align_bytes=64)
         ks = sb.tile([P, N], U8, name="ks", align_bytes=64)
+        cs = sb.tile([P, N], U8, name="cs", align_bytes=64)
+        kw = sb.tile([P, N], U32, name="kw", align_bytes=64)
         nc.vector.tensor_copy(ks[:], ks_all[:].indirect(offsets[:]))
+        nc.vector.tensor_copy(q_bf[:], q_raw[:].rearrange("p j w -> p w j"))
+        nc.vector.tensor_copy(cs[:], cs_all[:].indirect(offsets[:]))
+        nc.vector.quantize_mx(out=qw[:].bitcast(FP8X4), scales=qs[:], in_=q_bf[:].rearrange("p w j -> p (w j)"))
+        nc.vector.tensor_copy(c_plane[:].bitcast(I32), cs[:].bitcast(I32))
+        for r in range(4):
+            nc.sync.dma_start(k_plane[r:P:32, :].bitcast(I32), ks[8 * r : P : 32, :].bitcast(I32))
+        for r in range(1, 4):
+            nc.sync.dma_start(c_plane[4 + r : P : 32, :].bitcast(I32), cs[4 + 8 * r : P : 32, :].bitcast(I32))
         nc.vector.tensor_copy(kw[:], kw_all[:].bitcast(U32).indirect(offsets[:]))
 
-        a_ps = ps.tile([P, N], F32, name="a_ps")
-        nc.tensor.matmul_mx(out=a_ps[:], lhsT=qw[:].bitcast(FP8X4), lhsT_scale=qs[:],
-                            rhs=kw[:].bitcast(FP8X4), rhs_scale=ks[:], start=True, stop=True)
-        gate = sb.tile([P, N], F32, name="gate", align_bytes=64)
-        nc.scalar.activation(gate[:], a_ps[:], ACT.Silu)
-
-        def product(y, lo, width, cw):
-            z = ps.tile([P, width], F32, name=f"z{lo}")
-            at = lo % HALF
-            nc.tensor.matmul_mx(out=z[:], lhsT=qw[:].bitcast(FP8X4), lhsT_scale=qs[:],
-                                rhs=cw[:, at : at + width].bitcast(FP8X4), rhs_scale=cs[4:P, lo : lo + width], start=True, stop=True)
-            nc.scalar.copy(y[:, at : at + width], z[:])
-
         offs_h = [offsets[:, h * HALF // 16 : (h + 1) * HALF // 16] for h in range(2)]
-        cs = sb.tile([P, N], U8, name="cs", align_bytes=64)
-        cw0 = sb.tile([P, HALF], U32, name="cw0", align_bytes=64)
-        cw1 = sb.tile([P, HALF], U32, name="cw1", align_bytes=64)
-        y0 = sb.tile([P, HALF], F32, name="y0", align_bytes=64)
-        y1 = sb.tile([P, HALF], F32, name="y1", align_bytes=64)
-        nc.vector.tensor_copy(cs[:], cs_all[:].indirect(offsets[:]))
-        nc.vector.tensor_copy(cw0[:], cw_all[:].bitcast(U32).indirect(offs_h[0]))
-        nc.vector.tensor_copy(cw1[:], cw_all[:].bitcast(U32).indirect(offs_h[1]))
-        product(y0, 0, HALF // 2, cw0)
-        product(y0, HALF // 2, HALF // 2, cw0)
-        product(y1, HALF, HALF, cw1)
-        for h, y in enumerate((y0, y1)):
-            nc.vector.tensor_tensor(placed[:].indirect(offs_h[h]), gate[:, h * HALF : (h + 1) * HALF], y[:], mybir.AluOpType.mult)
+        cw = [sb.tile([P, HALF], U32, name=f"cw{h}", align_bytes=64) for h in range(2)]
+        gate = [sb.tile([P, HALF], F32, name=f"gate{h}", align_bytes=64) for h in range(2)]
+        y = [sb.tile([P, HALF], F32, name=f"y{h}", align_bytes=64) for h in range(2)]
+        for h in range(2):
+            nc.vector.tensor_copy(cw[h][:], cw_all[:].bitcast(U32).indirect(offs_h[h]))
+
+        def product(bank, words, scales):
+            acc = ps.tile([P, HALF], F32, name=bank)
+            width = words.shape[1]
+            nc.tensor.matmul_mx(out=acc[:, :width], lhsT=qw[:].bitcast(FP8X4), lhsT_scale=qs[:],
+                                rhs=words.bitcast(FP8X4), rhs_scale=scales, start=True, stop=True)
+            return acc[:, :width]
+
+        quarter = HALF // 2
+        nc.scalar.activation(gate[0][:], product("bank0", kw[:, :HALF], k_plane[:, :HALF]), ACT.Silu)
+        nc.scalar.copy(y[0][:, :quarter], product("bank1", cw[0][:, :quarter], c_plane[4:P, :quarter]))
+        nc.scalar.copy(y[0][:, quarter:], product("bank2", cw[0][:, quarter:], c_plane[4:P, quarter:HALF]))
+        nc.scalar.activation(gate[1][:], product("bank1", kw[:, HALF:], k_plane[:, HALF:]), ACT.Silu)
+        nc.scalar.copy(y[1][:], product("bank3", cw[1][:], c_plane[4:P, HALF:]))
+        for h in range(2):
+            nc.vector.tensor_tensor(placed[:].indirect(offs_h[h]), gate[h][:], y[h][:], mybir.AluOpType.mult)
 
         nc.sync.dma_start(out[0], placed[:])

@@ -49,7 +49,7 @@ def tile_attend_neu_swigluscat_topk_kernel(tc, qT, k_words, k_scales, c_words, c
         cs = sb.tile([P, N], U8, name="cs", align_bytes=64)
         kw = sb.tile([P, N], U32, name="kw", align_bytes=64)
         nc.vector.tensor_copy(ks[:], ks_all[:].indirect(offsets[:]))
-        nc.vector.tensor_copy(q_bf[:], q_raw[:].rearrange("p j w -> p w j"))
+        nc.scalar.copy(q_bf[:], q_raw[:].rearrange("p j w -> p w j"))
         nc.vector.tensor_copy(cs[:], cs_all[:].indirect(offsets[:]))
         nc.vector.quantize_mx(out=qw[:].bitcast(FP8X4), scales=qs[:], in_=q_bf[:].rearrange("p w j -> p (w j)"))
         nc.vector.tensor_copy(c_plane[:].bitcast(I32), cs[:].bitcast(I32))

@@ -4,7 +4,7 @@ import concourse.mybir as mybir
 
 P, PACK, T, N, NQ = 128, 4, 2048, 512, 128
 HALF = N // 2
-LEAD = T // 8
+LEAD = T // 4
 F32, BF16 = mybir.dt.float32, mybir.dt.bfloat16
 I32, U32, U16, U8 = mybir.dt.int32, mybir.dt.uint32, mybir.dt.uint16, mybir.dt.uint8
 FP8X4 = mybir.dt.float8_e4m3fn_x4
@@ -33,9 +33,9 @@ def tile_attend_neu_swigluscat_topk_kernel(tc, qT, k_words, k_scales, c_words, c
         nc.vector.memset(k_plane[:].bitcast(I32), 0)
         nc.vector.memset(placed[:], 0.0)
 
-        nc.sync.dma_start(offsets[:], offs)
         k_src = k_words[0].rearrange("p n t -> p (n t)").bitcast(I32)
         nc.sync.dma_start(kw_all[:, :LEAD], k_src[:, :LEAD])
+        nc.sync.dma_start(offsets[:], offs)
         nc.sync.dma_start(ks_all[0:P:8, :].bitcast(I32), k_scales[0].bitcast(I32))
         nc.sync.dma_start(q_raw[:], qT[0].rearrange("(p j) w -> p j w", j=PACK))
         nc.sync.dma_start(cs_all[4:P:8, :].bitcast(I32), c_scales[0].bitcast(I32))

@@ -4,7 +4,7 @@ import concourse.mybir as mybir
 
 P, PACK, T, N, NQ = 128, 4, 2048, 512, 128
 HALF = N // 2
-LEAD = T // 4
+LEAD = T // 2
 F32, BF16 = mybir.dt.float32, mybir.dt.bfloat16
 I32, U32, U16, U8 = mybir.dt.int32, mybir.dt.uint32, mybir.dt.uint16, mybir.dt.uint8
 FP8X4 = mybir.dt.float8_e4m3fn_x4
@@ -34,10 +34,10 @@ def tile_attend_neu_swigluscat_topk_kernel(tc, qT, k_words, k_scales, c_words, c
         nc.vector.memset(placed[:], 0.0)
 
         k_src = k_words[0].rearrange("p n t -> p (n t)").bitcast(I32)
-        nc.sync.dma_start(kw_all[:, :LEAD], k_src[:, :LEAD])
+        nc.sync.dma_start(q_raw[:], qT[0].rearrange("(p j) w -> p j w", j=PACK))
         nc.sync.dma_start(offsets[:], offs)
         nc.sync.dma_start(ks_all[0:P:8, :].bitcast(I32), k_scales[0].bitcast(I32))
-        nc.sync.dma_start(q_raw[:], qT[0].rearrange("(p j) w -> p j w", j=PACK))
+        nc.sync.dma_start(kw_all[:, :LEAD], k_src[:, :LEAD])
         nc.sync.dma_start(cs_all[4:P:8, :].bitcast(I32), c_scales[0].bitcast(I32))
         nc.sync.dma_start(kw_all[:, LEAD:], k_src[:, LEAD:])
         nc.sync.dma_start(cw_all[:], c_words[0].rearrange("p n t -> p (n t)").bitcast(I32))

@@ -16,11 +16,12 @@ def tile_attend_neu_swigluscat_topk_kernel(tc, qT, k_words, k_scales, c_words, c
     nc = tc.nc
     with ExitStack() as ctx:
         sb = ctx.enter_context(tc.tile_pool(name="sb", bufs=1))
+        reuse = ctx.enter_context(tc.tile_pool(name="reuse", bufs=1))
         ps = ctx.enter_context(tc.psum_pool(name="ps", bufs=1))
 
         offsets = sb.tile([P, N // 16], U16, name="offsets")
         ks_all = sb.tile([P, T], U8, name="ks_all", align_bytes=64)
-        cs_all = sb.tile([P, T], U8, name="cs_all", align_bytes=64)
+        cs_all = reuse.tile([P, T], U8, name="cs_all", tag="early", align_bytes=64)
         kw_all = sb.tile([P, T], I32, name="kw_all", align_bytes=64)
         q_raw = sb.tile([P, PACK, NQ], F32, name="q_raw", align_bytes=64)
         cw_all = sb.tile([P, T], I32, name="cw_all", align_bytes=64)
@@ -43,7 +44,7 @@ def tile_attend_neu_swigluscat_topk_kernel(tc, qT, k_words, k_scales, c_words, c
         nc.sync.dma_start(cw_all[:], c_words[0].rearrange("p n t -> p (n t)").bitcast(I32))
 
         q_bf = sb.tile([P, NQ, PACK], BF16, name="q_bf", align_bytes=64)
-        qw = sb.tile([P, NQ], U32, name="qw", align_bytes=64)
+        qw = reuse.tile([P, NQ], U32, name="qw", tag="early", align_bytes=64)
         qs = sb.tile([P, NQ], U8, name="qs", align_bytes=64)
         ks = sb.tile([P, N], U8, name="ks", align_bytes=64)
         cs = sb.tile([P, N], U8, name="cs", align_bytes=64)
@@ -51,8 +52,8 @@ def tile_attend_neu_swigluscat_topk_kernel(tc, qT, k_words, k_scales, c_words, c
         nc.vector.tensor_copy(ks[:], ks_all[:].indirect(offsets[:]))
         nc.scalar.copy(q_bf[:], q_raw[:].rearrange("p j w -> p w j"))
         nc.vector.tensor_copy(cs[:], cs_all[:].indirect(offsets[:]))
-        nc.vector.quantize_mx(out=qw[:].bitcast(FP8X4), scales=qs[:], in_=q_bf[:].rearrange("p w j -> p (w j)"))
         nc.vector.tensor_copy(c_plane[:].bitcast(I32), cs[:].bitcast(I32))
+        nc.vector.quantize_mx(out=qw[:].bitcast(FP8X4), scales=qs[:], in_=q_bf[:].rearrange("p w j -> p (w j)"))
         for r in range(4):
             nc.sync.dma_start(k_plane[r:P:32, :].bitcast(I32), ks[8 * r : P : 32, :].bitcast(I32))
         for r in range(1, 4):

@@ -4,7 +4,6 @@ import concourse.mybir as mybir
 
 P, PACK, T, N, NQ = 128, 4, 2048, 512, 128
 HALF = N // 2
-LEAD = T // 2
 F32, BF16 = mybir.dt.float32, mybir.dt.bfloat16
 I32, U32, U16, U8 = mybir.dt.int32, mybir.dt.uint32, mybir.dt.uint16, mybir.dt.uint8
 FP8X4 = mybir.dt.float8_e4m3fn_x4
@@ -16,12 +15,11 @@ def tile_attend_neu_swigluscat_topk_kernel(tc, qT, k_words, k_scales, c_words, c
     nc = tc.nc
     with ExitStack() as ctx:
         sb = ctx.enter_context(tc.tile_pool(name="sb", bufs=1))
-        reuse = ctx.enter_context(tc.tile_pool(name="reuse", bufs=1))
         ps = ctx.enter_context(tc.psum_pool(name="ps", bufs=1))
 
         offsets = sb.tile([P, N // 16], U16, name="offsets")
         ks_all = sb.tile([P, T], U8, name="ks_all", align_bytes=64)
-        cs_all = reuse.tile([P, T], U8, name="cs_all", tag="early", align_bytes=64)
+        cs_all = sb.tile([P, T], U8, name="cs_all", align_bytes=64)
         kw_all = sb.tile([P, T], I32, name="kw_all", align_bytes=64)
         q_raw = sb.tile([P, PACK, NQ], F32, name="q_raw", align_bytes=64)
         cw_all = sb.tile([P, T], I32, name="cw_all", align_bytes=64)
@@ -38,13 +36,12 @@ def tile_attend_neu_swigluscat_topk_kernel(tc, qT, k_words, k_scales, c_words, c
         nc.sync.dma_start(q_raw[:], qT[0].rearrange("(p j) w -> p j w", j=PACK))
         nc.sync.dma_start(offsets[:], offs)
         nc.sync.dma_start(ks_all[0:P:8, :].bitcast(I32), k_scales[0].bitcast(I32))
-        nc.sync.dma_start(kw_all[:, :LEAD], k_src[:, :LEAD])
         nc.sync.dma_start(cs_all[4:P:8, :].bitcast(I32), c_scales[0].bitcast(I32))
-        nc.sync.dma_start(kw_all[:, LEAD:], k_src[:, LEAD:])
+        nc.sync.dma_start(kw_all[:], k_src)
         nc.sync.dma_start(cw_all[:], c_words[0].rearrange("p n t -> p (n t)").bitcast(I32))
 
         q_bf = sb.tile([P, NQ, PACK], BF16, name="q_bf", align_bytes=64)
-        qw = reuse.tile([P, NQ], U32, name="qw", tag="early", align_bytes=64)
+        qw = sb.tile([P, NQ], U32, name="qw", align_bytes=64)
         qs = sb.tile([P, NQ], U8, name="qs", align_bytes=64)
         ks = sb.tile([P, N], U8, name="ks", align_bytes=64)
         cs = sb.tile([P, N], U8, name="cs", align_bytes=64)

@@ -4,6 +4,7 @@ import concourse.mybir as mybir
 
 P, PACK, T, N, NQ = 128, 4, 2048, 512, 128
 HALF = N // 2
+LEAD = 5 * T // 16
 F32, BF16 = mybir.dt.float32, mybir.dt.bfloat16
 I32, U32, U16, U8 = mybir.dt.int32, mybir.dt.uint32, mybir.dt.uint16, mybir.dt.uint8
 FP8X4 = mybir.dt.float8_e4m3fn_x4
@@ -33,11 +34,12 @@ def tile_attend_neu_swigluscat_topk_kernel(tc, qT, k_words, k_scales, c_words, c
         nc.vector.memset(placed[:], 0.0)
 
         k_src = k_words[0].rearrange("p n t -> p (n t)").bitcast(I32)
-        nc.sync.dma_start(q_raw[:], qT[0].rearrange("(p j) w -> p j w", j=PACK))
+        nc.sync.dma_start(kw_all[:, :LEAD], k_src[:, :LEAD])
         nc.sync.dma_start(offsets[:], offs)
         nc.sync.dma_start(ks_all[0:P:8, :].bitcast(I32), k_scales[0].bitcast(I32))
+        nc.sync.dma_start(q_raw[:], qT[0].rearrange("(p j) w -> p j w", j=PACK))
         nc.sync.dma_start(cs_all[4:P:8, :].bitcast(I32), c_scales[0].bitcast(I32))
-        nc.sync.dma_start(kw_all[:], k_src)
+        nc.sync.dma_start(kw_all[:, LEAD:], k_src[:, LEAD:])
         nc.sync.dma_start(cw_all[:], c_words[0].rearrange("p n t -> p (n t)").bitcast(I32))
 
         q_bf = sb.tile([P, NQ, PACK], BF16, name="q_bf", align_bytes=64)

@@ -36,7 +36,7 @@ def tile_attend_neu_swigluscat_topk_kernel(tc, qT, k_words, k_scales, c_words, c
         k_src = k_words[0].rearrange("p n t -> p (n t)").bitcast(I32)
         nc.sync.dma_start(kw_all[:, :LEAD], k_src[:, :LEAD])
         nc.sync.dma_start(offsets[:], offs)
-        nc.sync.dma_start(ks_all[0:P:8, :].bitcast(I32), k_scales[0].bitcast(I32))
+        nc.sync.dma_start(ks_all[11:117:7, :].bitcast(I32), k_scales[0].bitcast(I32))
         nc.sync.dma_start(q_raw[:], qT[0].rearrange("(p j) w -> p j w", j=PACK))
         nc.sync.dma_start(cs_all[4:P:8, :].bitcast(I32), c_scales[0].bitcast(I32))
         nc.sync.dma_start(kw_all[:, LEAD:], k_src[:, LEAD:])
@@ -54,7 +54,7 @@ def tile_attend_neu_swigluscat_topk_kernel(tc, qT, k_words, k_scales, c_words, c
         nc.vector.tensor_copy(c_plane[:].bitcast(I32), cs[:].bitcast(I32))
         nc.vector.quantize_mx(out=qw[:].bitcast(FP8X4), scales=qs[:], in_=q_bf[:].rearrange("p w j -> p (w j)"))
         for r in range(4):
-            nc.sync.dma_start(k_plane[r:P:32, :].bitcast(I32), ks[8 * r : P : 32, :].bitcast(I32))
+            nc.sync.dma_start(k_plane[r:P:32, :].bitcast(I32), ks[11 + 7 * r : 96 + 7 * r : 28, :].bitcast(I32))
         for r in range(1, 4):
             nc.sync.dma_start(c_plane[4 + r : P : 32, :].bitcast(I32), cs[4 + 8 * r : P : 32, :].bitcast(I32))
         nc.vector.tensor_copy(kw[:], kw_all[:].bitcast(U32).indirect(offsets[:]))

@@ -4,12 +4,14 @@ import concourse.mybir as mybir
 
 P, PACK, T, N, NQ = 128, 4, 2048, 512, 128
 HALF = N // 2
-LEAD = 5 * T // 16
+QUARTER = N // 4
 F32, BF16 = mybir.dt.float32, mybir.dt.bfloat16
 I32, U32, U16, U8 = mybir.dt.int32, mybir.dt.uint32, mybir.dt.uint16, mybir.dt.uint8
 FP8X4 = mybir.dt.float8_e4m3fn_x4
 ACT = mybir.ActivationFunctionType
 FLOPS = 2 * 2 * NQ * 512 * N
+LEAD = 5 * T // 16
+ROW0, ROW_STEP = 11, 7
 
 
 def tile_attend_neu_swigluscat_topk_kernel(tc, qT, k_words, k_scales, c_words, c_scales, offs, out):
@@ -22,47 +24,50 @@ def tile_attend_neu_swigluscat_topk_kernel(tc, qT, k_words, k_scales, c_words, c
         ks_all = sb.tile([P, T], U8, name="ks_all", align_bytes=64)
         cs_all = sb.tile([P, T], U8, name="cs_all", align_bytes=64)
         kw_all = sb.tile([P, T], I32, name="kw_all", align_bytes=64)
-        q_raw = sb.tile([P, PACK, NQ], F32, name="q_raw", align_bytes=64)
         cw_all = sb.tile([P, T], I32, name="cw_all", align_bytes=64)
+        q_raw = sb.tile([P, PACK, NQ], F32, name="q_raw", align_bytes=64)
         placed = sb.tile([P, T], F32, name="placed", align_bytes=64)
+        planes = [sb.tile([P, N], U8, name=f"planes{h}", align_bytes=64) for h in range(2)]
 
         nc.vector.memset(ks_all[:].bitcast(I32), 0)
         nc.vector.memset(cs_all[:].bitcast(I32), 0)
-        k_plane = sb.tile([P, N], U8, name="k_plane", align_bytes=64)
-        c_plane = sb.tile([P, N], U8, name="c_plane", align_bytes=64)
-        nc.vector.memset(k_plane[:].bitcast(I32), 0)
+        for h in range(2):
+            nc.vector.memset(planes[h][:].bitcast(I32), 0)
         nc.vector.memset(placed[:], 0.0)
 
+        staged = slice(ROW0, ROW0 + 15 * ROW_STEP + 1, ROW_STEP)
         k_src = k_words[0].rearrange("p n t -> p (n t)").bitcast(I32)
         nc.sync.dma_start(kw_all[:, :LEAD], k_src[:, :LEAD])
         nc.sync.dma_start(offsets[:], offs)
-        nc.sync.dma_start(ks_all[11:117:7, :].bitcast(I32), k_scales[0].bitcast(I32))
+        nc.sync.dma_start(ks_all[staged, :].bitcast(I32), k_scales[0].bitcast(I32))
         nc.sync.dma_start(q_raw[:], qT[0].rearrange("(p j) w -> p j w", j=PACK))
-        nc.sync.dma_start(cs_all[4:P:8, :].bitcast(I32), c_scales[0].bitcast(I32))
+        nc.sync.dma_start(cs_all[staged, :].bitcast(I32), c_scales[0].bitcast(I32))
         nc.sync.dma_start(kw_all[:, LEAD:], k_src[:, LEAD:])
         nc.sync.dma_start(cw_all[:], c_words[0].rearrange("p n t -> p (n t)").bitcast(I32))
 
         q_bf = sb.tile([P, NQ, PACK], BF16, name="q_bf", align_bytes=64)
         qw = sb.tile([P, NQ], U32, name="qw", align_bytes=64)
         qs = sb.tile([P, NQ], U8, name="qs", align_bytes=64)
-        ks = sb.tile([P, N], U8, name="ks", align_bytes=64)
-        cs = sb.tile([P, N], U8, name="cs", align_bytes=64)
+        picked = [sb.tile([P, N], U8, name=f"picked{h}", align_bytes=64) for h in range(2)]
+        offs_h = [offsets[:, h * HALF // 16 : (h + 1) * HALF // 16] for h in range(2)]
         kw = sb.tile([P, N], U32, name="kw", align_bytes=64)
-        nc.vector.tensor_copy(ks[:], ks_all[:].indirect(offsets[:]))
         nc.scalar.copy(q_bf[:], q_raw[:].rearrange("p j w -> p w j"))
-        nc.vector.tensor_copy(cs[:], cs_all[:].indirect(offsets[:]))
-        nc.vector.tensor_copy(c_plane[:].bitcast(I32), cs[:].bitcast(I32))
+        for h in range(2):
+            nc.vector.tensor_copy(picked[h][:, :HALF], ks_all[:].indirect(offs_h[h]))
+        for h in range(2):
+            nc.vector.tensor_copy(picked[h][:, HALF:], cs_all[:].indirect(offs_h[h]))
+            for r in range(4):
+                first = ROW0 + ROW_STEP * r
+                nc.sync.dma_start(
+                    planes[h][r:P:32, :].bitcast(I32),
+                    picked[h][first : first + 12 * ROW_STEP + 1 : 4 * ROW_STEP, :].bitcast(I32),
+                )
         nc.vector.quantize_mx(out=qw[:].bitcast(FP8X4), scales=qs[:], in_=q_bf[:].rearrange("p w j -> p (w j)"))
-        for r in range(4):
-            nc.sync.dma_start(k_plane[r:P:32, :].bitcast(I32), ks[11 + 7 * r : 96 + 7 * r : 28, :].bitcast(I32))
-        for r in range(1, 4):
-            nc.sync.dma_start(c_plane[4 + r : P : 32, :].bitcast(I32), cs[4 + 8 * r : P : 32, :].bitcast(I32))
         nc.vector.tensor_copy(kw[:], kw_all[:].bitcast(U32).indirect(offsets[:]))
 
-        offs_h = [offsets[:, h * HALF // 16 : (h + 1) * HALF // 16] for h in range(2)]
         cw = [sb.tile([P, HALF], U32, name=f"cw{h}", align_bytes=64) for h in range(2)]
         gate = [sb.tile([P, HALF], F32, name=f"gate{h}", align_bytes=64) for h in range(2)]
-        y = [sb.tile([P, HALF], F32, name=f"y{h}", align_bytes=64) for h in range(2)]
+        z = [sb.tile([P, HALF], F32, name=f"z{h}", align_bytes=64) for h in range(2)]
         for h in range(2):
             nc.vector.tensor_copy(cw[h][:], cw_all[:].bitcast(U32).indirect(offs_h[h]))
 
@@ -73,13 +78,12 @@ def tile_attend_neu_swigluscat_topk_kernel(tc, qT, k_words, k_scales, c_words, c
                                 rhs=words.bitcast(FP8X4), rhs_scale=scales, start=True, stop=True)
             return acc[:, :width]
 
-        quarter = HALF // 2
-        nc.scalar.activation(gate[0][:], product("bank0", kw[:, :HALF], k_plane[:, :HALF]), ACT.Silu)
-        nc.scalar.copy(y[0][:, :quarter], product("bank1", cw[0][:, :quarter], c_plane[4:P, :quarter]))
-        nc.scalar.copy(y[0][:, quarter:], product("bank2", cw[0][:, quarter:], c_plane[4:P, quarter:HALF]))
-        nc.scalar.activation(gate[1][:], product("bank1", kw[:, HALF:], k_plane[:, HALF:]), ACT.Silu)
-        nc.scalar.copy(y[1][:], product("bank3", cw[1][:], c_plane[4:P, HALF:]))
+        nc.scalar.activation(gate[0][:], product("bank0", kw[:, :HALF], planes[0][:, :HALF]), ACT.Silu)
+        nc.scalar.copy(z[0][:, :QUARTER], product("bank1", cw[0][:, :QUARTER], planes[0][:, HALF : HALF + QUARTER]))
+        nc.scalar.copy(z[0][:, QUARTER:], product("bank2", cw[0][:, QUARTER:], planes[0][:, HALF + QUARTER :]))
+        nc.scalar.activation(gate[1][:], product("bank1", kw[:, HALF:], planes[1][:, :HALF]), ACT.Silu)
+        nc.scalar.copy(z[1][:], product("bank3", cw[1][:], planes[1][:, HALF:]))
         for h in range(2):
-            nc.vector.tensor_tensor(placed[:].indirect(offs_h[h]), gate[h][:], y[h][:], mybir.AluOpType.mult)
+            nc.vector.tensor_tensor(placed[:].indirect(offs_h[h]), gate[h][:], z[h][:], mybir.AluOpType.mult)
 
         nc.sync.dma_start(out[0], placed[:])

@@ -78,7 +78,8 @@ def tile_attend_neu_swigluscat_topk_kernel(tc, qT, k_words, k_scales, c_words, c
                                 rhs=words.bitcast(FP8X4), rhs_scale=scales, start=True, stop=True)
             return acc[:, :width]
 
-        nc.scalar.activation(gate[0][:], product("bank0", kw[:, :HALF], planes[0][:, :HALF]), ACT.Silu)
+        nc.scalar.activation(gate[0][:, :QUARTER], product("bank0", kw[:, :QUARTER], planes[0][:, :QUARTER]), ACT.Silu)
+        nc.scalar.activation(gate[0][:, QUARTER:], product("bank4", kw[:, QUARTER:HALF], planes[0][:, QUARTER:HALF]), ACT.Silu)
         nc.scalar.copy(z[0][:, :QUARTER], product("bank1", cw[0][:, :QUARTER], planes[0][:, HALF : HALF + QUARTER]))
         nc.scalar.copy(z[0][:, QUARTER:], product("bank2", cw[0][:, QUARTER:], planes[0][:, HALF + QUARTER :]))
         nc.scalar.activation(gate[1][:], product("bank1", kw[:, HALF:], planes[1][:, :HALF]), ACT.Silu)

@@ -10,7 +10,6 @@ I32, U32, U16, U8 = mybir.dt.int32, mybir.dt.uint32, mybir.dt.uint16, mybir.dt.u
 FP8X4 = mybir.dt.float8_e4m3fn_x4
 ACT = mybir.ActivationFunctionType
 FLOPS = 2 * 2 * NQ * 512 * N
-LEAD = 5 * T // 16
 ROW0, ROW_STEP = 11, 7
 
 
@@ -37,12 +36,12 @@ def tile_attend_neu_swigluscat_topk_kernel(tc, qT, k_words, k_scales, c_words, c
 
         staged = slice(ROW0, ROW0 + 15 * ROW_STEP + 1, ROW_STEP)
         k_src = k_words[0].rearrange("p n t -> p (n t)").bitcast(I32)
-        nc.sync.dma_start(kw_all[:, :LEAD], k_src[:, :LEAD])
+        nc.sync.dma_start(kw_all[0:P:2, :], k_src[0:P:2, :])
         nc.sync.dma_start(offsets[:], offs)
         nc.sync.dma_start(ks_all[staged, :].bitcast(I32), k_scales[0].bitcast(I32))
         nc.sync.dma_start(q_raw[:], qT[0].rearrange("(p j) w -> p j w", j=PACK))
         nc.sync.dma_start(cs_all[staged, :].bitcast(I32), c_scales[0].bitcast(I32))
-        nc.sync.dma_start(kw_all[:, LEAD:], k_src[:, LEAD:])
+        nc.sync.dma_start(kw_all[1:P:2, :], k_src[1:P:2, :])
         nc.sync.dma_start(cw_all[:], c_words[0].rearrange("p n t -> p (n t)").bitcast(I32))
 
         q_bf = sb.tile([P, NQ, PACK], BF16, name="q_bf", align_bytes=64)

@@ -20,12 +20,12 @@ def tile_attend_neu_swigluscat_topk_kernel(tc, qT, k_words, k_scales, c_words, c
         ps = ctx.enter_context(tc.psum_pool(name="ps", bufs=1))
 
         offsets = sb.tile([P, N // 16], U16, name="offsets")
-        ks_all = sb.tile([P, T], U8, name="ks_all", align_bytes=64)
-        cs_all = sb.tile([P, T], U8, name="cs_all", align_bytes=64)
-        kw_all = sb.tile([P, T], I32, name="kw_all", align_bytes=64)
-        cw_all = sb.tile([P, T], I32, name="cw_all", align_bytes=64)
-        q_raw = sb.tile([P, PACK, NQ], F32, name="q_raw", align_bytes=64)
-        placed = sb.tile([P, T], F32, name="placed", align_bytes=64)
+        ks_all = sb.tile([P, T], U8, name="ks_all", align_bytes=256)
+        cs_all = sb.tile([P, T], U8, name="cs_all", align_bytes=256)
+        kw_all = sb.tile([P, T], I32, name="kw_all", align_bytes=256)
+        cw_all = sb.tile([P, T], I32, name="cw_all", align_bytes=256)
+        q_raw = sb.tile([P, PACK, NQ], F32, name="q_raw", align_bytes=256)
+        placed = sb.tile([P, T], F32, name="placed", align_bytes=256)
         planes = [sb.tile([P, N], U8, name=f"planes{h}", align_bytes=64) for h in range(2)]
 
         nc.vector.memset(ks_all[:].bitcast(I32), 0)

@@ -9,8 +9,10 @@ F32, BF16 = mybir.dt.float32, mybir.dt.bfloat16
 I32, U32, U16, U8 = mybir.dt.int32, mybir.dt.uint32, mybir.dt.uint16, mybir.dt.uint8
 FP8X4 = mybir.dt.float8_e4m3fn_x4
 ACT = mybir.ActivationFunctionType
+MULT, ADD = mybir.AluOpType.mult, mybir.AluOpType.add
 FLOPS = 2 * 2 * NQ * 512 * N
 ROW0, ROW_STEP = 11, 7
+STORE_WIDTHS = (320, 384, 384, 448, 512)
 
 
 def tile_attend_neu_swigluscat_topk_kernel(tc, qT, k_words, k_scales, c_words, c_scales, offs, out):
@@ -25,50 +27,44 @@ def tile_attend_neu_swigluscat_topk_kernel(tc, qT, k_words, k_scales, c_words, c
         kw_all = sb.tile([P, T], I32, name="kw_all", align_bytes=256)
         cw_all = sb.tile([P, T], I32, name="cw_all", align_bytes=256)
         q_raw = sb.tile([P, PACK, NQ], F32, name="q_raw", align_bytes=256)
-        placed = sb.tile([P, T], F32, name="placed", align_bytes=256)
-        planes = [sb.tile([P, N], U8, name=f"planes{h}", align_bytes=64) for h in range(2)]
+        placed = [sb.tile([P, T], F32, name=f"placed{h}", align_bytes=256) for h in range(2)]
+        planes = sb.tile([P, 2 * N], U8, name="planes", align_bytes=64)
 
         nc.vector.memset(ks_all[:].bitcast(I32), 0)
         nc.vector.memset(cs_all[:].bitcast(I32), 0)
+        nc.vector.memset(planes[:].bitcast(I32), 0)
         for h in range(2):
-            nc.vector.memset(planes[h][:].bitcast(I32), 0)
-        nc.vector.memset(placed[:], 0.0)
+            nc.vector.memset(placed[h][:], 0.0)
 
         staged = slice(ROW0, ROW0 + 15 * ROW_STEP + 1, ROW_STEP)
         k_src = k_words[0].rearrange("p n t -> p (n t)").bitcast(I32)
         nc.sync.dma_start(kw_all[0:P:2, :], k_src[0:P:2, :])
         nc.sync.dma_start(offsets[:], offs)
         nc.sync.dma_start(ks_all[staged, :].bitcast(I32), k_scales[0].bitcast(I32))
-        nc.sync.dma_start(q_raw[:], qT[0].rearrange("(p j) w -> p j w", j=PACK))
         nc.sync.dma_start(cs_all[staged, :].bitcast(I32), c_scales[0].bitcast(I32))
+        nc.sync.dma_start(q_raw[:], qT[0].rearrange("(p j) w -> p j w", j=PACK))
         nc.sync.dma_start(kw_all[1:P:2, :], k_src[1:P:2, :])
         nc.sync.dma_start(cw_all[:], c_words[0].rearrange("p n t -> p (n t)").bitcast(I32))
 
         q_bf = sb.tile([P, NQ, PACK], BF16, name="q_bf", align_bytes=64)
         qw = sb.tile([P, NQ], U32, name="qw", align_bytes=64)
         qs = sb.tile([P, NQ], U8, name="qs", align_bytes=64)
-        picked = [sb.tile([P, N], U8, name=f"picked{h}", align_bytes=64) for h in range(2)]
-        offs_h = [offsets[:, h * HALF // 16 : (h + 1) * HALF // 16] for h in range(2)]
+        picked = sb.tile([P, 2 * N], U8, name="picked", align_bytes=64)
         kw = sb.tile([P, N], U32, name="kw", align_bytes=64)
         nc.scalar.copy(q_bf[:], q_raw[:].rearrange("p j w -> p w j"))
-        for h in range(2):
-            nc.vector.tensor_copy(picked[h][:, :HALF], ks_all[:].indirect(offs_h[h]))
-        for h in range(2):
-            nc.vector.tensor_copy(picked[h][:, HALF:], cs_all[:].indirect(offs_h[h]))
-            for r in range(4):
-                first = ROW0 + ROW_STEP * r
-                nc.sync.dma_start(
-                    planes[h][r:P:32, :].bitcast(I32),
-                    picked[h][first : first + 12 * ROW_STEP + 1 : 4 * ROW_STEP, :].bitcast(I32),
-                )
+        nc.vector.tensor_copy(picked[:, :N], ks_all[:].indirect(offsets[:]))
+        nc.vector.tensor_copy(picked[:, N:], cs_all[:].indirect(offsets[:]))
+        for r in range(4):
+            first = ROW0 + ROW_STEP * r
+            nc.sync.dma_start(
+                planes[r:P:32, :].bitcast(I32),
+                picked[first : first + 12 * ROW_STEP + 1 : 4 * ROW_STEP, :].bitcast(I32),
+            )
         nc.vector.quantize_mx(out=qw[:].bitcast(FP8X4), scales=qs[:], in_=q_bf[:].rearrange("p w j -> p (w j)"))
         nc.vector.tensor_copy(kw[:], kw_all[:].bitcast(U32).indirect(offsets[:]))
 
-        cw = [sb.tile([P, HALF], U32, name=f"cw{h}", align_bytes=64) for h in range(2)]
-        gate = [sb.tile([P, HALF], F32, name=f"gate{h}", align_bytes=64) for h in range(2)]
-        z = [sb.tile([P, HALF], F32, name=f"z{h}", align_bytes=64) for h in range(2)]
-        for h in range(2):
-            nc.vector.tensor_copy(cw[h][:], cw_all[:].bitcast(U32).indirect(offs_h[h]))
+        def listed(first, width):
+            return offsets[:, first // 16 : (first + width) // 16]
 
         def product(bank, words, scales):
             acc = ps.tile([P, HALF], F32, name=bank)
@@ -77,13 +73,30 @@ def tile_attend_neu_swigluscat_topk_kernel(tc, qT, k_words, k_scales, c_words, c
                                 rhs=words.bitcast(FP8X4), rhs_scale=scales, start=True, stop=True)
             return acc[:, :width]
 
-        nc.scalar.activation(gate[0][:, :QUARTER], product("bank0", kw[:, :QUARTER], planes[0][:, :QUARTER]), ACT.Silu)
-        nc.scalar.activation(gate[0][:, QUARTER:], product("bank4", kw[:, QUARTER:HALF], planes[0][:, QUARTER:HALF]), ACT.Silu)
-        nc.scalar.copy(z[0][:, :QUARTER], product("bank1", cw[0][:, :QUARTER], planes[0][:, HALF : HALF + QUARTER]))
-        nc.scalar.copy(z[0][:, QUARTER:], product("bank2", cw[0][:, QUARTER:], planes[0][:, HALF + QUARTER :]))
-        nc.scalar.activation(gate[1][:], product("bank1", kw[:, HALF:], planes[1][:, :HALF]), ACT.Silu)
-        nc.scalar.copy(z[1][:], product("bank3", cw[1][:], planes[1][:, HALF:]))
-        for h in range(2):
-            nc.vector.tensor_tensor(placed[:].indirect(offs_h[h]), gate[h][:], z[h][:], mybir.AluOpType.mult)
+        zeros = sb.tile([P, QUARTER], F32, name="zeros", align_bytes=64)
+        nc.vector.memset(zeros[:], 0.0)
+        cw = sb.tile([P, N], U32, name="cw", align_bytes=64)
+        gate = sb.tile([P, N], F32, name="gate", align_bytes=64)
+        y = sb.tile([P, N], F32, name="y", align_bytes=64)
+        for first, width in ((0, HALF), (HALF, QUARTER), (HALF + QUARTER, QUARTER)):
+            nc.vector.tensor_copy(cw[:, first : first + width], cw_all[:].bitcast(U32).indirect(listed(first, width)))
 
-        nc.sync.dma_start(out[0], placed[:])
+        for h in range(2):
+            cols = slice(h * HALF, (h + 1) * HALF)
+            nc.scalar.activation(gate[:, cols], product(f"a{h}", kw[:, cols], planes[:, cols]), ACT.Silu)
+        for j in range(4):
+            cols = slice(j * QUARTER, (j + 1) * QUARTER)
+            z = product(f"z{j}", cw[:, cols], planes[:, N + j * QUARTER : N + (j + 1) * QUARTER])
+            nc.vector.tensor_tensor(y[:, cols], z, gate[:, cols], MULT)
+        nc.scalar.activation(placed[0][:].indirect(listed(0, HALF)), y[:, :HALF], ACT.Copy)
+        for j in range(2, 4):
+            cols = slice(j * QUARTER, (j + 1) * QUARTER)
+            nc.vector.tensor_tensor(placed[1][:].indirect(listed(j * QUARTER, QUARTER)), y[:, cols], zeros[:], ADD)
+
+        first = 0
+        for i, width in enumerate(STORE_WIDTHS):
+            cols = slice(first, first + width)
+            merged = sb.tile([P, width], F32, name=f"merged{i}", align_bytes=256)
+            nc.vector.tensor_tensor(merged[:], placed[0][:, cols], placed[1][:, cols], ADD)
+            nc.sync.dma_start(out[0][:, cols], merged[:])
+            first = first + width

@@ -12,6 +12,7 @@ ACT = mybir.ActivationFunctionType
 MULT, ADD = mybir.AluOpType.mult, mybir.AluOpType.add
 FLOPS = 2 * 2 * NQ * 512 * N
 ROW0, ROW_STEP = 11, 7
+SCALAR_SHARE = 288
 STORE_WIDTHS = (320, 384, 384, 448, 512)
 
 
@@ -28,7 +29,7 @@ def tile_attend_neu_swigluscat_topk_kernel(tc, qT, k_words, k_scales, c_words, c
         cw_all = sb.tile([P, T], I32, name="cw_all", align_bytes=256)
         q_raw = sb.tile([P, PACK, NQ], F32, name="q_raw", align_bytes=256)
         placed = [sb.tile([P, T], F32, name=f"placed{h}", align_bytes=256) for h in range(2)]
-        planes = sb.tile([P, 2 * N], U8, name="planes", align_bytes=64)
+        planes = sb.tile([P, 2 * N], U8, name="planes", align_bytes=256)
 
         nc.vector.memset(ks_all[:].bitcast(I32), 0)
         nc.vector.memset(cs_all[:].bitcast(I32), 0)
@@ -49,17 +50,25 @@ def tile_attend_neu_swigluscat_topk_kernel(tc, qT, k_words, k_scales, c_words, c
         q_bf = sb.tile([P, NQ, PACK], BF16, name="q_bf", align_bytes=64)
         qw = sb.tile([P, NQ], U32, name="qw", align_bytes=64)
         qs = sb.tile([P, NQ], U8, name="qs", align_bytes=64)
-        picked = sb.tile([P, 2 * N], U8, name="picked", align_bytes=64)
+        picked = sb.tile([P, 2 * N], U8, name="picked", align_bytes=256)
         kw = sb.tile([P, N], U32, name="kw", align_bytes=64)
         nc.scalar.copy(q_bf[:], q_raw[:].rearrange("p j w -> p w j"))
-        nc.vector.tensor_copy(picked[:, :N], ks_all[:].indirect(offsets[:]))
-        nc.vector.tensor_copy(picked[:, N:], cs_all[:].indirect(offsets[:]))
-        for r in range(4):
+
+        def move_rows(r, cols):
             first = ROW0 + ROW_STEP * r
             nc.sync.dma_start(
-                planes[r:P:32, :].bitcast(I32),
-                picked[first : first + 12 * ROW_STEP + 1 : 4 * ROW_STEP, :].bitcast(I32),
+                planes[r:P:32, cols].bitcast(I32),
+                picked[first : first + 12 * ROW_STEP + 1 : 4 * ROW_STEP, cols].bitcast(I32),
             )
+
+        nc.vector.tensor_copy(picked[:, :N], ks_all[:].indirect(offsets[:]))
+        nc.vector.tensor_copy(picked[:, N : N + HALF], cs_all[:].indirect(offsets[:, : HALF // 16]))
+        for r in range(1, 4):
+            move_rows(r, slice(0, N + HALF))
+        nc.vector.tensor_copy(picked[:, N + HALF :], cs_all[:].indirect(offsets[:, HALF // 16 :]))
+        move_rows(0, slice(0, 2 * N))
+        for r in range(1, 4):
+            move_rows(r, slice(N + HALF, 2 * N))
         nc.vector.quantize_mx(out=qw[:].bitcast(FP8X4), scales=qs[:], in_=q_bf[:].rearrange("p w j -> p (w j)"))
         nc.vector.tensor_copy(kw[:], kw_all[:].bitcast(U32).indirect(offsets[:]))
 
@@ -73,7 +82,7 @@ def tile_attend_neu_swigluscat_topk_kernel(tc, qT, k_words, k_scales, c_words, c
                                 rhs=words.bitcast(FP8X4), rhs_scale=scales, start=True, stop=True)
             return acc[:, :width]
 
-        zeros = sb.tile([P, QUARTER], F32, name="zeros", align_bytes=64)
+        zeros = sb.tile([P, N - SCALAR_SHARE], F32, name="zeros", align_bytes=64)
         nc.vector.memset(zeros[:], 0.0)
         cw = sb.tile([P, N], U32, name="cw", align_bytes=64)
         gate = sb.tile([P, N], F32, name="gate", align_bytes=64)
@@ -81,17 +90,19 @@ def tile_attend_neu_swigluscat_topk_kernel(tc, qT, k_words, k_scales, c_words, c
         for first, width in ((0, HALF), (HALF, QUARTER), (HALF + QUARTER, QUARTER)):
             nc.vector.tensor_copy(cw[:, first : first + width], cw_all[:].bitcast(U32).indirect(listed(first, width)))
 
-        for h in range(2):
-            cols = slice(h * HALF, (h + 1) * HALF)
-            nc.scalar.activation(gate[:, cols], product(f"a{h}", kw[:, cols], planes[:, cols]), ACT.Silu)
+        for first, width in ((0, QUARTER), (QUARTER, QUARTER), (HALF, HALF)):
+            cols = slice(first, first + width)
+            nc.scalar.activation(gate[:, cols], product(f"a{first}", kw[:, cols], planes[:, cols]), ACT.Silu)
         for j in range(4):
-            cols = slice(j * QUARTER, (j + 1) * QUARTER)
-            z = product(f"z{j}", cw[:, cols], planes[:, N + j * QUARTER : N + (j + 1) * QUARTER])
-            nc.vector.tensor_tensor(y[:, cols], z, gate[:, cols], MULT)
-        nc.scalar.activation(placed[0][:].indirect(listed(0, HALF)), y[:, :HALF], ACT.Copy)
-        for j in range(2, 4):
-            cols = slice(j * QUARTER, (j + 1) * QUARTER)
-            nc.vector.tensor_tensor(placed[1][:].indirect(listed(j * QUARTER, QUARTER)), y[:, cols], zeros[:], ADD)
+            first = j * QUARTER
+            z = product(f"z{j}", cw[:, first : first + QUARTER], planes[:, N + first : N + first + QUARTER])
+            cuts = [0, SCALAR_SHARE - first, QUARTER] if first < SCALAR_SHARE < first + QUARTER else [0, QUARTER]
+            for lo, hi in zip(cuts, cuts[1:]):
+                nc.vector.tensor_tensor(y[:, first + lo : first + hi], z[:, lo:hi], gate[:, first + lo : first + hi], MULT)
+        nc.scalar.activation(placed[0][:].indirect(listed(0, SCALAR_SHARE)), y[:, :SCALAR_SHARE], ACT.Copy)
+        nc.vector.tensor_tensor(
+            placed[1][:].indirect(listed(SCALAR_SHARE, N - SCALAR_SHARE)), y[:, SCALAR_SHARE:], zeros[:], ADD
+        )
 
         first = 0
         for i, width in enumerate(STORE_WIDTHS):

@@ -13,7 +13,7 @@ MULT, ADD = mybir.AluOpType.mult, mybir.AluOpType.add
 FLOPS = 2 * 2 * NQ * 512 * N
 ROW0, ROW_STEP = 11, 7
 SCALAR_SHARE = 288
-STORE_WIDTHS = (320, 384, 384, 448, 512)
+STORE_WIDTHS = (256, 320, 384, 384, 384, 320)
 
 
 def tile_attend_neu_swigluscat_topk_kernel(tc, qT, k_words, k_scales, c_words, c_scales, offs, out):
@@ -82,8 +82,6 @@ def tile_attend_neu_swigluscat_topk_kernel(tc, qT, k_words, k_scales, c_words, c
                                 rhs=words.bitcast(FP8X4), rhs_scale=scales, start=True, stop=True)
             return acc[:, :width]
 
-        zeros = sb.tile([P, N - SCALAR_SHARE], F32, name="zeros", align_bytes=64)
-        nc.vector.memset(zeros[:], 0.0)
         cw = sb.tile([P, N], U32, name="cw", align_bytes=64)
         gate = sb.tile([P, N], F32, name="gate", align_bytes=64)
         y = sb.tile([P, N], F32, name="y", align_bytes=64)
@@ -98,10 +96,12 @@ def tile_attend_neu_swigluscat_topk_kernel(tc, qT, k_words, k_scales, c_words, c
             z = product(f"z{j}", cw[:, first : first + QUARTER], planes[:, N + first : N + first + QUARTER])
             cuts = [0, SCALAR_SHARE - first, QUARTER] if first < SCALAR_SHARE < first + QUARTER else [0, QUARTER]
             for lo, hi in zip(cuts, cuts[1:]):
-                nc.vector.tensor_tensor(y[:, first + lo : first + hi], z[:, lo:hi], gate[:, first + lo : first + hi], MULT)
+                cols = slice(first + lo, first + hi)
+                factor = 1.0 if first + lo < SCALAR_SHARE else 0.5
+                nc.vector.scalar_tensor_tensor(y[:, cols], z[:, lo:hi], factor, gate[:, cols], MULT, MULT)
         nc.scalar.activation(placed[0][:].indirect(listed(0, SCALAR_SHARE)), y[:, :SCALAR_SHARE], ACT.Copy)
         nc.vector.tensor_tensor(
-            placed[1][:].indirect(listed(SCALAR_SHARE, N - SCALAR_SHARE)), y[:, SCALAR_SHARE:], zeros[:], ADD
+            placed[1][:].indirect(listed(SCALAR_SHARE, N - SCALAR_SHARE)), y[:, SCALAR_SHARE:], y[:, SCALAR_SHARE:], ADD
         )
 
         first = 0

from contextlib import ExitStack

import concourse.mybir as mybir

P, PACK, T, N, NQ = 128, 4, 2048, 512, 128
HALF = N // 2
QUARTER = N // 4
F32, BF16 = mybir.dt.float32, mybir.dt.bfloat16
I32, U32, U16, U8 = mybir.dt.int32, mybir.dt.uint32, mybir.dt.uint16, mybir.dt.uint8
FP8X4 = mybir.dt.float8_e4m3fn_x4
ACT = mybir.ActivationFunctionType
MULT, ADD = mybir.AluOpType.mult, mybir.AluOpType.add
FLOPS = 2 * 2 * NQ * 512 * N
ROW0, ROW_STEP = 11, 7
SCALAR_SHARE = 288
STORE_WIDTHS = (256, 320, 384, 384, 384, 320)


def tile_attend_neu_swigluscat_topk_kernel(tc, qT, k_words, k_scales, c_words, c_scales, offs, out):
    nc = tc.nc
    with ExitStack() as ctx:
        sb = ctx.enter_context(tc.tile_pool(name="sb", bufs=1))
        ps = ctx.enter_context(tc.psum_pool(name="ps", bufs=1))

        offsets = sb.tile([P, N // 16], U16, name="offsets")
        ks_all = sb.tile([P, T], U8, name="ks_all", align_bytes=256)
        cs_all = sb.tile([P, T], U8, name="cs_all", align_bytes=256)
        kw_all = sb.tile([P, T], I32, name="kw_all", align_bytes=256)
        cw_all = sb.tile([P, T], I32, name="cw_all", align_bytes=256)
        q_raw = sb.tile([P, PACK, NQ], F32, name="q_raw", align_bytes=256)
        placed = [sb.tile([P, T], F32, name=f"placed{h}", align_bytes=256) for h in range(2)]
        planes = sb.tile([P, 2 * N], U8, name="planes", align_bytes=256)

        nc.vector.memset(ks_all[:].bitcast(I32), 0)
        nc.vector.memset(cs_all[:].bitcast(I32), 0)
        nc.vector.memset(planes[:].bitcast(I32), 0)
        for h in range(2):
            nc.vector.memset(placed[h][:], 0.0)

        staged = slice(ROW0, ROW0 + 15 * ROW_STEP + 1, ROW_STEP)
        k_src = k_words[0].rearrange("p n t -> p (n t)").bitcast(I32)
        nc.sync.dma_start(kw_all[0:P:2, :], k_src[0:P:2, :])
        nc.sync.dma_start(offsets[:], offs)
        nc.sync.dma_start(ks_all[staged, :].bitcast(I32), k_scales[0].bitcast(I32))
        nc.sync.dma_start(cs_all[staged, :].bitcast(I32), c_scales[0].bitcast(I32))
        nc.sync.dma_start(q_raw[:], qT[0].rearrange("(p j) w -> p j w", j=PACK))
        nc.sync.dma_start(kw_all[1:P:2, :], k_src[1:P:2, :])
        nc.sync.dma_start(cw_all[:], c_words[0].rearrange("p n t -> p (n t)").bitcast(I32))

        q_bf = sb.tile([P, NQ, PACK], BF16, name="q_bf", align_bytes=64)
        qw = sb.tile([P, NQ], U32, name="qw", align_bytes=64)
        qs = sb.tile([P, NQ], U8, name="qs", align_bytes=64)
        picked = sb.tile([P, 2 * N], U8, name="picked", align_bytes=256)
        kw = sb.tile([P, N], U32, name="kw", align_bytes=64)
        nc.scalar.copy(q_bf[:], q_raw[:].rearrange("p j w -> p w j"))

        def move_rows(r, cols):
            first = ROW0 + ROW_STEP * r
            nc.sync.dma_start(
                planes[r:P:32, cols].bitcast(I32),
                picked[first : first + 12 * ROW_STEP + 1 : 4 * ROW_STEP, cols].bitcast(I32),
            )

        nc.vector.tensor_copy(picked[:, :N], ks_all[:].indirect(offsets[:]))
        nc.vector.tensor_copy(picked[:, N : N + HALF], cs_all[:].indirect(offsets[:, : HALF // 16]))
        for r in range(1, 4):
            move_rows(r, slice(0, N + HALF))
        nc.vector.tensor_copy(picked[:, N + HALF :], cs_all[:].indirect(offsets[:, HALF // 16 :]))
        move_rows(0, slice(0, 2 * N))
        for r in range(1, 4):
            move_rows(r, slice(N + HALF, 2 * N))
        nc.vector.quantize_mx(out=qw[:].bitcast(FP8X4), scales=qs[:], in_=q_bf[:].rearrange("p w j -> p (w j)"))
        nc.vector.tensor_copy(kw[:], kw_all[:].bitcast(U32).indirect(offsets[:]))

        def listed(first, width):
            return offsets[:, first // 16 : (first + width) // 16]

        def product(bank, words, scales):
            acc = ps.tile([P, HALF], F32, name=bank)
            width = words.shape[1]
            nc.tensor.matmul_mx(out=acc[:, :width], lhsT=qw[:].bitcast(FP8X4), lhsT_scale=qs[:],
                                rhs=words.bitcast(FP8X4), rhs_scale=scales, start=True, stop=True)
            return acc[:, :width]

        cw = sb.tile([P, N], U32, name="cw", align_bytes=64)
        gate = sb.tile([P, N], F32, name="gate", align_bytes=64)
        y = sb.tile([P, N], F32, name="y", align_bytes=64)
        for first, width in ((0, HALF), (HALF, QUARTER), (HALF + QUARTER, QUARTER)):
            nc.vector.tensor_copy(cw[:, first : first + width], cw_all[:].bitcast(U32).indirect(listed(first, width)))

        for first, width in ((0, QUARTER), (QUARTER, QUARTER), (HALF, HALF)):
            cols = slice(first, first + width)
            nc.scalar.activation(gate[:, cols], product(f"a{first}", kw[:, cols], planes[:, cols]), ACT.Silu)
        for j in range(4):
            first = j * QUARTER
            z = product(f"z{j}", cw[:, first : first + QUARTER], planes[:, N + first : N + first + QUARTER])
            cuts = [0, SCALAR_SHARE - first, QUARTER] if first < SCALAR_SHARE < first + QUARTER else [0, QUARTER]
            for lo, hi in zip(cuts, cuts[1:]):
                cols = slice(first + lo, first + hi)
                factor = 1.0 if first + lo < SCALAR_SHARE else 0.5
                nc.vector.scalar_tensor_tensor(y[:, cols], z[:, lo:hi], factor, gate[:, cols], MULT, MULT)
        nc.scalar.activation(placed[0][:].indirect(listed(0, SCALAR_SHARE)), y[:, :SCALAR_SHARE], ACT.Copy)
        nc.vector.tensor_tensor(
            placed[1][:].indirect(listed(SCALAR_SHARE, N - SCALAR_SHARE)), y[:, SCALAR_SHARE:], y[:, SCALAR_SHARE:], ADD
        )

        first = 0
        for i, width in enumerate(STORE_WIDTHS):
            cols = slice(first, first + width)
            merged = sb.tile([P, width], F32, name=f"merged{i}", align_bytes=256)
            nc.vector.tensor_tensor(merged[:], placed[0][:, cols], placed[1][:, cols], ADD)
            nc.sync.dma_start(out[0][:, cols], merged[:])
            first = first + width
